import numpy as np
import ml_dtypes


def mxq(x, axis, fmt="e4m3"):
    dtype, down = {"e4m3": (ml_dtypes.float8_e4m3fn, 7), "e5m2": (ml_dtypes.float8_e5m2, 14)}[fmt]
    v = np.moveaxis(np.asarray(x, np.float32).astype(ml_dtypes.bfloat16).astype(np.float64), axis, -1)
    blocks = v.reshape(v.shape[:-1] + (-1, 32))
    amax = np.abs(blocks).max(-1, keepdims=True)
    byte = np.maximum(np.where(amax > 0, np.frexp(amax)[1] - 1 + 127, 0) - down, 1)
    scale = np.exp2(byte - 127.0)
    codes = (blocks / scale).astype(np.float32).astype(dtype).astype(np.float64)
    return np.moveaxis((codes * scale).reshape(v.shape), -1, axis)


WIDE = False


def mx_kscale(k):
    if not WIDE:
        return np.ones(k)
    levels = np.array([10, -10, 5, -5, 0])
    if k % 512:
        return np.exp2(np.random.permutation(np.resize(levels, k // 32))).repeat(32)
    a = np.empty((k // 512, 16))
    for p in range(k // 512):
        a[p, :8] = np.random.permutation(np.resize(levels, 8))
        for g in range(8):
            far = levels[np.abs(levels - a[p, g]) >= 10]
            a[p, g + 8] = far[np.random.randint(len(far))]
    return np.exp2(a.ravel()).repeat(32)


def f64(x):
    return np.asarray(x).astype(np.float64)


def striped(idx):
    return np.tile(idx.reshape(-1, 16).T, (8, 1)).astype(np.uint16)


def unstriped(offs):
    return offs[:16].T.reshape(-1).astype(np.int64)


K, T, S, H, N = 1024, 2048, 1024, 512, 128


def setup_inputs():
    n = np.random.standard_normal
    s = mx_kscale(K)[:, None]
    u = mx_kscale(H)
    return {
        "xT": (n((K, T)) * s).astype(np.float32),
        "w1": (n((K, H)) / np.sqrt(K) / s * u).astype(np.float32),
        "w2": (n((H, N)) / np.sqrt(H) / u[:, None]).astype(np.float32),
        "pos": (0.5 * n((H, S)) * u[:, None]).astype(np.float32),
        "offs": striped(np.random.permutation(T)[(T * np.random.uniform(0, 1, S) ** 4).astype(np.int64)]),
    }


def reference(xT, w1, w2, pos, offs):
    xq = mxq(f64(xT)[:, unstriped(offs)], 0, "e4m3")
    h = (mxq(f64(w1), 0, "e4m3").T @ xq) + f64(pos)
    return mxq(f64(w2), 0, "e4m3").T @ mxq(h, 0, "e4m3")

@@ -1,0 +1,206 @@
+from contextlib import ExitStack
+
+import concourse.mybir as mybir
+
+K, T, S, H, N = 1024, 2048, 1024, 512, 128
+FLOPS = 2 * K * H * S + 2 * H * N * S
+
+F32 = mybir.dt.float32
+BF16 = mybir.dt.bfloat16
+U32 = mybir.dt.uint32
+U16 = mybir.dt.uint16
+U8 = mybir.dt.uint8
+FP8X4 = mybir.dt.float8_e4m3fn_x4
+ADD = mybir.AluOpType.add
+COPY = mybir.ActivationFunctionType.Copy
+
+P = 128
+PACK = 4
+K_PASS = P * PACK
+CHUNK = 128
+GROUP = 16
+RUN = 4
+
+X_LOADS = [
+    (0, 0, 1024, 512),
+    (0, 1024, 1536, 0),
+    (0, 1536, 2048, 336),
+    (1, 0, 512, 0),
+    (1, 512, 1024, 0),
+    (1, 1024, 1536, 336),
+    (1, 1536, 1792, 0),
+    (1, 1792, 2048, 168),
+]
+HALF = S // 2
+POS_PIECES = [(0, 512), (512, 1024)]
+OUT_PIECES = [(0, 256), (256, 512), (512, 768), (768, 896), (896, 1024)]
+
+
+def tile_picked_embpos_none_e_kernel(tc, xT, w1, w2, pos, offs, out):
+    nc = tc.nc
+    with ExitStack() as ctx:
+        keep = ctx.enter_context(tc.tile_pool(name="keep", bufs=1))
+        h_banks = ctx.enter_context(tc.psum_pool(name="h_banks", bufs=6))
+        out_banks = ctx.enter_context(tc.psum_pool(name="out_banks", bufs=2))
+
+        def tile(shape, dtype, name, tag=""):
+            return keep.tile(shape, dtype, name=name, tag=tag or name, align_bytes=64)
+
+        def quantize(values, name):
+            width = values.shape[1] // PACK
+            codes = tile([P, width], U32, name + "_codes")
+            scales = tile([P, width], U8, name + "_scales")
+            nc.vector.quantize_mx(out=codes[:].bitcast(FP8X4), scales=scales[:], in_=values)
+            return codes, scales
+
+        def scalar_copy(out, in_):
+            nc.scalar.activation(out=out, in_=in_, func=COPY)
+
+        def side_by_side(ap):
+            return ap.rearrange("p (c i j) -> p c j i", i=RUN, j=PACK)
+
+        def row_by_row(ap):
+            return ap.rearrange("p j (c i) -> p c j i", i=RUN)
+
+        offsets = tile([P, S // GROUP], U16, "offsets")
+        x_raw = []
+        for n, (z, lo, hi, share) in enumerate(X_LOADS):
+            raw = tile([P, PACK, hi - lo], F32, "x_raw%d" % n)
+            rows = xT[z * K_PASS : (z + 1) * K_PASS, :].rearrange("(p j) w -> p j w", j=PACK)
+            nc.sync.dma_start(out=raw[:], in_=rows[:, :, lo:hi])
+            x_raw.append(raw)
+            if n == 0:
+                nc.sync.dma_start(offsets[:], offs)
+        w1_raw = {}
+        for z in range(2):
+            rows = w1[z * K_PASS : (z + 1) * K_PASS, :].rearrange("(p j) c -> p j c", j=PACK)
+            for half in range(2):
+                raw = tile([P, PACK, H // 2], F32, "w1_raw%d%d" % (z, half))
+                nc.sync.dma_start(out=raw[:], in_=rows[:, :, half * H // 2 : (half + 1) * H // 2])
+                w1_raw[z, half] = raw
+        pos_rows = pos.rearrange("(p t) s -> p t s", t=PACK)
+        pos_sb = []
+        for n, (lo, hi) in enumerate(POS_PIECES):
+            piece = tile([P, PACK, hi - lo], F32, "pos%d" % n)
+            nc.sync.dma_start(out=piece[:], in_=pos_rows[:, :, lo:hi])
+            pos_sb.append(piece)
+            if n == 0:
+                w2_raw = tile([P, PACK, N], F32, "w2_raw")
+                nc.sync.dma_start(out=w2_raw[:], in_=w2.rearrange("(p j) c -> p j c", j=PACK))
+
+        all_codes = [tile([P, T], U32, "all_codes%d" % z) for z in range(2)]
+        all_scales = tile([P, T], U8, "all_scales")
+        nc.gpsimd.memset(all_scales[:], 0)
+
+        def round_x(n):
+            z, lo, hi, share = X_LOADS[n]
+            rounded = tile([P, PACK * (hi - lo)], BF16, "x_rounded%d" % n)
+            if share < hi - lo:
+                scalar_copy(side_by_side(rounded[:, PACK * share :]), row_by_row(x_raw[n][:, :, share:]))
+            if share > 0:
+                nc.vector.tensor_copy(
+                    out=side_by_side(rounded[:, : PACK * share]), in_=row_by_row(x_raw[n][:, :, :share])
+                )
+            return rounded
+
+        def quantize_x(n, rounded):
+            z, lo, hi, share = X_LOADS[n]
+            nc.vector.quantize_mx(
+                out=all_codes[z][:, lo:hi].bitcast(FP8X4), scales=all_scales[PACK * z :, lo:hi], in_=rounded[:]
+            )
+
+        def gather(window, dtype, lo, hi, name, tag=""):
+            picked = tile([P, hi - lo], dtype, name, tag)
+            nc.vector.tensor_copy(out=picked[:], in_=window[:].indirect(offsets[:, lo // GROUP : hi // GROUP]))
+            return picked
+
+        for n in range(3):
+            quantize_x(n, round_x(n))
+        codes0 = gather(all_codes[0], U32, 0, S, "codes0")
+        for n in range(3, 6):
+            quantize_x(n, round_x(n))
+        before_last = round_x(6)
+        last = round_x(7)
+        quantize_x(6, before_last)
+        quantize_x(7, last)
+        codes1 = [gather(all_codes[1], U32, 0, HALF, "codes1_0")]
+        x_scales = [gather(all_scales, U8, 0, HALF, "scales_0")]
+
+        def quantize_w1(z):
+            grouped = [tile([P, 2 * P * PACK], BF16, "w1_grouped%d%d" % (z, pair)) for pair in range(2)]
+            for half in range(2):
+                for pair in range(2):
+                    scalar_copy(
+                        grouped[pair][:].rearrange("p (t m j) -> p m j t", t=2, j=PACK)[:, half * P // 2 : (half + 1) * P // 2],
+                        w1_raw[z, half][:].rearrange("p j (m t) -> p m j t", t=PACK)[:, :, :, 2 * pair : 2 * pair + 2],
+                    )
+            return [quantize(grouped[pair][:], "w1_%d%d" % (z, pair)) for pair in range(2)]
+
+        w1_mx = [quantize_w1(0)]
+        codes1.append(gather(all_codes[1], U32, HALF, S, "codes1_1", tag="w1_raw01"))
+        w1_mx.append(quantize_w1(1))
+        x_scales.append(gather(all_scales, U8, HALF, S, "scales_1", tag="w1_raw11"))
+
+        w2_grouped = tile([P, N * PACK], BF16, "w2_grouped")
+        scalar_copy(side_by_side(w2_grouped[:]), row_by_row(w2_raw[:]))
+        w2_codes, w2_scales = quantize(w2_grouped[:], "w2")
+
+        def find(pieces, col):
+            return [n for n, (lo, hi) in enumerate(pieces) if lo <= col < hi][0]
+
+        h_tiles = [tile([P, PACK * (hi - lo)], BF16, "h%d" % lo) for lo, hi in OUT_PIECES]
+
+        def first_layer(c):
+            first = c * CHUNK
+            bank = h_banks.tile([P, PACK, CHUNK], F32, name="h_bank")
+            half, at = divmod(first, HALF)
+            x_codes = [codes0[:, first : first + CHUNK], codes1[half][:, at : at + CHUNK]]
+            for t in range(PACK):
+                for z in range(2):
+                    w_codes, w_scales = w1_mx[z][t // 2]
+                    m = slice((t % 2) * P, (t % 2 + 1) * P)
+                    nc.tensor.matmul_mx(
+                        out=bank[:, t, :],
+                        lhsT=w_codes[:, m].bitcast(FP8X4),
+                        lhsT_scale=w_scales[:, m],
+                        rhs=x_codes[z].bitcast(FP8X4),
+                        rhs_scale=x_scales[half][PACK * z :, at : at + CHUNK],
+                        start=(z == 0),
+                        stop=(z == 1),
+                    )
+            np_ = find(POS_PIECES, first)
+            at_pos = first - POS_PIECES[np_][0]
+            no = find(OUT_PIECES, first)
+            at_h = PACK * (first - OUT_PIECES[no][0])
+            nc.vector.tensor_tensor(
+                out=side_by_side(h_tiles[no][:, at_h : at_h + PACK * CHUNK]),
+                in0=row_by_row(bank[:]),
+                in1=row_by_row(pos_sb[np_][:, :, at_pos : at_pos + CHUNK]),
+                op=ADD,
+            )
+
+        def second_layer(no):
+            lo, hi = OUT_PIECES[no]
+            codes, scales = quantize(h_tiles[no][:], "h%d" % lo)
+            bank = out_banks.tile([P, hi - lo], F32, name="out_bank")
+            nc.tensor.matmul_mx(
+                out=bank[:],
+                lhsT=w2_codes[:].bitcast(FP8X4),
+                lhsT_scale=w2_scales[:],
+                rhs=codes[:].bitcast(FP8X4),
+                rhs_scale=scales[:],
+                start=True,
+                stop=True,
+            )
+            result = tile([P, hi - lo], F32, "result%d" % lo)
+            nc.scalar.copy(out=result[:], in_=bank[:])
+            nc.sync.dma_start(out=out[:, lo:hi], in_=result[:])
+
+        done = 0
+        for c in range(S // CHUNK):
+            first_layer(c)
+            if OUT_PIECES[done][1] <= c * CHUNK:
+                second_layer(done)
+                done = done + 1
+        for no in range(done, len(OUT_PIECES)):
+            second_layer(no)

@@ -19,20 +19,20 @@ PACK = 4
 K_PASS = P * PACK
 CHUNK = 128
 GROUP = 16
-RUN = 4
+RUN = 2
 
 X_LOADS = [
     (0, 0, 1024, 512),
     (0, 1024, 1536, 0),
     (0, 1536, 2048, 336),
     (1, 0, 512, 0),
-    (1, 512, 1024, 0),
+    (1, 512, 1024, 336),
     (1, 1024, 1536, 336),
     (1, 1536, 1792, 0),
     (1, 1792, 2048, 168),
 ]
-HALF = S // 2
-POS_PIECES = [(0, 512), (512, 1024)]
+POS_PIECES = [(0, 256), (256, 512), (512, 768), (768, 1024)]
+CODE_PIECES = [(0, 768), (768, 1024)]
 OUT_PIECES = [(0, 256), (256, 512), (512, 768), (768, 896), (896, 1024)]
 
 
@@ -40,8 +40,7 @@ def tile_picked_embpos_none_e_kernel(tc, xT, w1, w2, pos, offs, out):
     nc = tc.nc
     with ExitStack() as ctx:
         keep = ctx.enter_context(tc.tile_pool(name="keep", bufs=1))
-        h_banks = ctx.enter_context(tc.psum_pool(name="h_banks", bufs=6))
-        out_banks = ctx.enter_context(tc.psum_pool(name="out_banks", bufs=2))
+        banks = ctx.enter_context(tc.psum_pool(name="banks", bufs=8))
 
         def tile(shape, dtype, name, tag=""):
             return keep.tile(shape, dtype, name=name, tag=tag or name, align_bytes=64)
@@ -123,8 +122,7 @@ def tile_picked_embpos_none_e_kernel(tc, xT, w1, w2, pos, offs, out):
         last = round_x(7)
         quantize_x(6, before_last)
         quantize_x(7, last)
-        codes1 = [gather(all_codes[1], U32, 0, HALF, "codes1_0")]
-        x_scales = [gather(all_scales, U8, 0, HALF, "scales_0")]
+        x_scales = gather(all_scales, U8, 0, S, "scales")
 
         def quantize_w1(z):
             grouped = [tile([P, 2 * P * PACK], BF16, "w1_grouped%d%d" % (z, pair)) for pair in range(2)]
@@ -137,9 +135,9 @@ def tile_picked_embpos_none_e_kernel(tc, xT, w1, w2, pos, offs, out):
             return [quantize(grouped[pair][:], "w1_%d%d" % (z, pair)) for pair in range(2)]
 
         w1_mx = [quantize_w1(0)]
-        codes1.append(gather(all_codes[1], U32, HALF, S, "codes1_1", tag="w1_raw01"))
+        codes1 = [gather(all_codes[1], U32, *CODE_PIECES[0], "codes1_0", tag="w1_raw01")]
         w1_mx.append(quantize_w1(1))
-        x_scales.append(gather(all_scales, U8, HALF, S, "scales_1", tag="w1_raw11"))
+        codes1.append(gather(all_codes[1], U32, *CODE_PIECES[1], "codes1_1", tag="w1_raw11"))
 
         w2_grouped = tile([P, N * PACK], BF16, "w2_grouped")
         scalar_copy(side_by_side(w2_grouped[:]), row_by_row(w2_raw[:]))
@@ -152,8 +150,9 @@ def tile_picked_embpos_none_e_kernel(tc, xT, w1, w2, pos, offs, out):
 
         def first_layer(c):
             first = c * CHUNK
-            bank = h_banks.tile([P, PACK, CHUNK], F32, name="h_bank")
-            half, at = divmod(first, HALF)
+            bank = banks.tile([P, PACK, CHUNK], F32, name="bank")
+            half = find(CODE_PIECES, first)
+            at = first - CODE_PIECES[half][0]
             x_codes = [codes0[:, first : first + CHUNK], codes1[half][:, at : at + CHUNK]]
             for t in range(PACK):
                 for z in range(2):
@@ -164,10 +163,14 @@ def tile_picked_embpos_none_e_kernel(tc, xT, w1, w2, pos, offs, out):
                         lhsT=w_codes[:, m].bitcast(FP8X4),
                         lhsT_scale=w_scales[:, m],
                         rhs=x_codes[z].bitcast(FP8X4),
-                        rhs_scale=x_scales[half][PACK * z :, at : at + CHUNK],
+                        rhs_scale=x_scales[PACK * z :, first : first + CHUNK],
                         start=(z == 0),
                         stop=(z == 1),
                     )
+            return bank
+
+        def add_pos(c, bank):
+            first = c * CHUNK
             np_ = find(POS_PIECES, first)
             at_pos = first - POS_PIECES[np_][0]
             no = find(OUT_PIECES, first)
@@ -182,7 +185,7 @@ def tile_picked_embpos_none_e_kernel(tc, xT, w1, w2, pos, offs, out):
         def second_layer(no):
             lo, hi = OUT_PIECES[no]
             codes, scales = quantize(h_tiles[no][:], "h%d" % lo)
-            bank = out_banks.tile([P, hi - lo], F32, name="out_bank")
+            bank = banks.tile([P, hi - lo], F32, name="bank")
             nc.tensor.matmul_mx(
                 out=bank[:],
                 lhsT=w2_codes[:].bitcast(FP8X4),
@@ -194,11 +197,13 @@ def tile_picked_embpos_none_e_kernel(tc, xT, w1, w2, pos, offs, out):
             )
             result = tile([P, hi - lo], F32, "result%d" % lo)
             nc.scalar.copy(out=result[:], in_=bank[:])
-            nc.sync.dma_start(out=out[:, lo:hi], in_=result[:])
+            queue = nc.scalar if hi == S else nc.sync
+            queue.dma_start(out=out[:, lo:hi], in_=result[:])
 
+        h_sums = [first_layer(c) for c in range(S // CHUNK)]
         done = 0
         for c in range(S // CHUNK):
-            first_layer(c)
+            add_pos(c, h_sums[c])
             if OUT_PIECES[done][1] <= c * CHUNK:
                 second_layer(done)
                 done = done + 1

@@ -8,6 +8,7 @@ FLOPS = 2 * K * H * S + 2 * H * N * S
 F32 = mybir.dt.float32
 BF16 = mybir.dt.bfloat16
 U32 = mybir.dt.uint32
+I32 = mybir.dt.int32
 U16 = mybir.dt.uint16
 U8 = mybir.dt.uint8
 FP8X4 = mybir.dt.float8_e4m3fn_x4
@@ -20,19 +21,15 @@ K_PASS = P * PACK
 CHUNK = 128
 GROUP = 16
 RUN = 2
+LEAD = 3
 
 X_LOADS = [
-    (0, 0, 1024, 512),
-    (0, 1024, 1536, 0),
-    (0, 1536, 2048, 336),
-    (1, 0, 512, 0),
-    (1, 512, 1024, 336),
-    (1, 1024, 1536, 336),
-    (1, 1536, 1792, 0),
-    (1, 1792, 2048, 168),
+    [(0, 1024, 0), (1024, 2048, 672)],
+    [(0, 1024, 0), (1024, 2048, 672)],
+    [(0, 1024, 0), (1024, 2048, 288)],
+    [(0, 1024, 0), (1024, 1536, 512), (1536, 2048, 288)],
 ]
-POS_PIECES = [(0, 256), (256, 512), (512, 768), (768, 1024)]
-CODE_PIECES = [(0, 768), (768, 1024)]
+POS_PIECES = [(0, 512), (512, 768), (768, 1024)]
 OUT_PIECES = [(0, 256), (256, 512), (512, 768), (768, 896), (896, 1024)]
 
 
@@ -40,14 +37,15 @@ def tile_picked_embpos_none_e_kernel(tc, xT, w1, w2, pos, offs, out):
     nc = tc.nc
     with ExitStack() as ctx:
         keep = ctx.enter_context(tc.tile_pool(name="keep", bufs=1))
-        banks = ctx.enter_context(tc.psum_pool(name="banks", bufs=8))
+        banks = ctx.enter_context(tc.psum_pool(name="banks", bufs=LEAD))
+        out_banks = ctx.enter_context(tc.psum_pool(name="out_banks", bufs=4))
 
         def tile(shape, dtype, name, tag=""):
             return keep.tile(shape, dtype, name=name, tag=tag or name, align_bytes=64)
 
-        def quantize(values, name):
+        def quantize(values, name, tag=""):
             width = values.shape[1] // PACK
-            codes = tile([P, width], U32, name + "_codes")
+            codes = tile([P, width], U32, name + "_codes", tag)
             scales = tile([P, width], U8, name + "_scales")
             nc.vector.quantize_mx(out=codes[:].bitcast(FP8X4), scales=scales[:], in_=values)
             return codes, scales
@@ -55,92 +53,85 @@ def tile_picked_embpos_none_e_kernel(tc, xT, w1, w2, pos, offs, out):
         def scalar_copy(out, in_):
             nc.scalar.activation(out=out, in_=in_, func=COPY)
 
-        def side_by_side(ap):
-            return ap.rearrange("p (c i j) -> p c j i", i=RUN, j=PACK)
+        def side_by_side(ap, rows):
+            return ap.rearrange("p (c i j) -> p c j i", i=RUN, j=rows)
 
         def row_by_row(ap):
             return ap.rearrange("p j (c i) -> p c j i", i=RUN)
 
         offsets = tile([P, S // GROUP], U16, "offsets")
         x_raw = []
-        for n, (z, lo, hi, share) in enumerate(X_LOADS):
-            raw = tile([P, PACK, hi - lo], F32, "x_raw%d" % n)
-            rows = xT[z * K_PASS : (z + 1) * K_PASS, :].rearrange("(p j) w -> p j w", j=PACK)
-            nc.sync.dma_start(out=raw[:], in_=rows[:, :, lo:hi])
-            x_raw.append(raw)
+        for n, pieces in enumerate(X_LOADS):
+            z, u = divmod(n, 2)
+            rows = xT[z * K_PASS : (z + 1) * K_PASS, :].rearrange("(p j) w -> p j w", j=PACK)[:, 2 * u : 2 * u + 2, :]
+            raws = []
+            for lo, hi, share in pieces:
+                raw = tile([P, 2, hi - lo], F32, "x_raw%d_%d" % (n, lo))
+                nc.sync.dma_start(out=raw[:], in_=rows[:, :, lo:hi])
+                raws.append(raw)
+            x_raw.append(raws)
             if n == 0:
                 nc.sync.dma_start(offsets[:], offs)
-        w1_raw = {}
+        w1_raw = []
         for z in range(2):
-            rows = w1[z * K_PASS : (z + 1) * K_PASS, :].rearrange("(p j) c -> p j c", j=PACK)
-            for half in range(2):
-                raw = tile([P, PACK, H // 2], F32, "w1_raw%d%d" % (z, half))
-                nc.sync.dma_start(out=raw[:], in_=rows[:, :, half * H // 2 : (half + 1) * H // 2])
-                w1_raw[z, half] = raw
+            raw = tile([P, PACK, H], F32, "w1_raw%d" % z)
+            nc.sync.dma_start(out=raw[:], in_=w1[z * K_PASS : (z + 1) * K_PASS, :].rearrange("(p j) c -> p j c", j=PACK))
+            w1_raw.append(raw)
+        w2_raw = tile([P, PACK, N], F32, "w2_raw")
+        nc.sync.dma_start(out=w2_raw[:], in_=w2.rearrange("(p j) c -> p j c", j=PACK))
         pos_rows = pos.rearrange("(p t) s -> p t s", t=PACK)
         pos_sb = []
         for n, (lo, hi) in enumerate(POS_PIECES):
             piece = tile([P, PACK, hi - lo], F32, "pos%d" % n)
             nc.sync.dma_start(out=piece[:], in_=pos_rows[:, :, lo:hi])
             pos_sb.append(piece)
-            if n == 0:
-                w2_raw = tile([P, PACK, N], F32, "w2_raw")
-                nc.sync.dma_start(out=w2_raw[:], in_=w2.rearrange("(p j) c -> p j c", j=PACK))
 
-        all_codes = [tile([P, T], U32, "all_codes%d" % z) for z in range(2)]
-        all_scales = tile([P, T], U8, "all_scales")
-        nc.gpsimd.memset(all_scales[:], 0)
+        def round_pair(n):
+            pairs = tile([P, 2 * T], BF16, "pairs%d" % n)
+            for raw, (lo, hi, share) in zip(x_raw[n], X_LOADS[n]):
+                if share < hi - lo:
+                    scalar_copy(side_by_side(pairs[:, 2 * (lo + share) : 2 * hi], 2), row_by_row(raw[:, :, share:]))
+                if share > 0:
+                    nc.vector.tensor_copy(
+                        out=side_by_side(pairs[:, 2 * lo : 2 * (lo + share)], 2), in_=row_by_row(raw[:, :, :share])
+                    )
+            return pairs
 
-        def round_x(n):
-            z, lo, hi, share = X_LOADS[n]
-            rounded = tile([P, PACK * (hi - lo)], BF16, "x_rounded%d" % n)
-            if share < hi - lo:
-                scalar_copy(side_by_side(rounded[:, PACK * share :]), row_by_row(x_raw[n][:, :, share:]))
-            if share > 0:
+        halves = [(0, S // 2), (S // 2, S)]
+
+        def weave_x(z):
+            picked = [tile([P, 2, hi - lo], U32, "picked%d_%d" % (z, lo)) for lo, hi in halves]
+            for u in range(2):
+                pairs = round_pair(2 * z + u)
+                for (lo, hi), into in zip(halves, picked):
+                    nc.vector.tensor_copy(
+                        out=into[:, u, :], in_=pairs[:].bitcast(U32).indirect(offsets[:, lo // GROUP : hi // GROUP])
+                    )
+            woven = [tile([P, PACK * (hi - lo)], BF16, "woven%d_%d" % (z, lo)) for lo, hi in halves]
+            for into, words in zip(woven, picked):
                 nc.vector.tensor_copy(
-                    out=side_by_side(rounded[:, : PACK * share]), in_=row_by_row(x_raw[n][:, :, :share])
+                    out=side_by_side(into[:].bitcast(I32), 2), in_=row_by_row(words[:].bitcast(I32))
                 )
-            return rounded
+            return woven
 
-        def quantize_x(n, rounded):
-            z, lo, hi, share = X_LOADS[n]
-            nc.vector.quantize_mx(
-                out=all_codes[z][:, lo:hi].bitcast(FP8X4), scales=all_scales[PACK * z :, lo:hi], in_=rounded[:]
-            )
-
-        def gather(window, dtype, lo, hi, name, tag=""):
-            picked = tile([P, hi - lo], dtype, name, tag)
-            nc.vector.tensor_copy(out=picked[:], in_=window[:].indirect(offsets[:, lo // GROUP : hi // GROUP]))
-            return picked
-
-        for n in range(3):
-            quantize_x(n, round_x(n))
-        codes0 = gather(all_codes[0], U32, 0, S, "codes0")
-        for n in range(3, 6):
-            quantize_x(n, round_x(n))
-        before_last = round_x(6)
-        last = round_x(7)
-        quantize_x(6, before_last)
-        quantize_x(7, last)
-        x_scales = gather(all_scales, U8, 0, S, "scales")
+        x_mx = [[quantize(values[:], "x0_%d" % n) for n, values in enumerate(weave_x(0))]]
+        woven1 = weave_x(1)
 
         def quantize_w1(z):
             grouped = [tile([P, 2 * P * PACK], BF16, "w1_grouped%d%d" % (z, pair)) for pair in range(2)]
-            for half in range(2):
-                for pair in range(2):
-                    scalar_copy(
-                        grouped[pair][:].rearrange("p (t m j) -> p m j t", t=2, j=PACK)[:, half * P // 2 : (half + 1) * P // 2],
-                        w1_raw[z, half][:].rearrange("p j (m t) -> p m j t", t=PACK)[:, :, :, 2 * pair : 2 * pair + 2],
-                    )
+            for pair in range(2):
+                dealt = grouped[pair][:].rearrange("p (t m j) -> p m j t", t=2, j=PACK)
+                source = w1_raw[z][:].rearrange("p j (m t) -> p m j t", t=PACK)[:, :, :, 2 * pair : 2 * pair + 2]
+                scalar_copy(dealt, source)
             return [quantize(grouped[pair][:], "w1_%d%d" % (z, pair)) for pair in range(2)]
 
         w1_mx = [quantize_w1(0)]
-        codes1 = [gather(all_codes[1], U32, *CODE_PIECES[0], "codes1_0", tag="w1_raw01")]
+        x_mx.append([quantize(woven1[0][:], "x1_0", "w1_raw0")])
         w1_mx.append(quantize_w1(1))
-        codes1.append(gather(all_codes[1], U32, *CODE_PIECES[1], "codes1_1", tag="w1_raw11"))
+        x_mx[1].append(quantize(woven1[1][:], "x1_1", "w1_grouped11"))
 
         w2_grouped = tile([P, N * PACK], BF16, "w2_grouped")
-        scalar_copy(side_by_side(w2_grouped[:]), row_by_row(w2_raw[:]))
+        scalar_copy(side_by_side(w2_grouped[:], PACK), row_by_row(w2_raw[:]))
         w2_codes, w2_scales = quantize(w2_grouped[:], "w2")
 
         def find(pieces, col):
@@ -148,26 +139,21 @@ def tile_picked_embpos_none_e_kernel(tc, xT, w1, w2, pos, offs, out):
 
         h_tiles = [tile([P, PACK * (hi - lo)], BF16, "h%d" % lo) for lo, hi in OUT_PIECES]
 
-        def first_layer(c):
-            first = c * CHUNK
-            bank = banks.tile([P, PACK, CHUNK], F32, name="bank")
-            half = find(CODE_PIECES, first)
-            at = first - CODE_PIECES[half][0]
-            x_codes = [codes0[:, first : first + CHUNK], codes1[half][:, at : at + CHUNK]]
+        def first_layer_pass(c, z, bank):
+            half, at = divmod(c * CHUNK, S // 2)
+            x_codes, x_scales = x_mx[z][half]
             for t in range(PACK):
-                for z in range(2):
-                    w_codes, w_scales = w1_mx[z][t // 2]
-                    m = slice((t % 2) * P, (t % 2 + 1) * P)
-                    nc.tensor.matmul_mx(
-                        out=bank[:, t, :],
-                        lhsT=w_codes[:, m].bitcast(FP8X4),
-                        lhsT_scale=w_scales[:, m],
-                        rhs=x_codes[z].bitcast(FP8X4),
-                        rhs_scale=x_scales[PACK * z :, first : first + CHUNK],
-                        start=(z == 0),
-                        stop=(z == 1),
-                    )
-            return bank
+                w_codes, w_scales = w1_mx[z][t // 2]
+                m = slice((t % 2) * P, (t % 2 + 1) * P)
+                nc.tensor.matmul_mx(
+                    out=bank[:, t, :],
+                    lhsT=w_codes[:, m].bitcast(FP8X4),
+                    lhsT_scale=w_scales[:, m],
+                    rhs=x_codes[:, at : at + CHUNK].bitcast(FP8X4),
+                    rhs_scale=x_scales[:, at : at + CHUNK],
+                    start=(z == 0 and t == 0),
+                    stop=(z == 1 and t == PACK - 1),
+                )
 
         def add_pos(c, bank):
             first = c * CHUNK
@@ -176,7 +162,7 @@ def tile_picked_embpos_none_e_kernel(tc, xT, w1, w2, pos, offs, out):
             no = find(OUT_PIECES, first)
             at_h = PACK * (first - OUT_PIECES[no][0])
             nc.vector.tensor_tensor(
-                out=side_by_side(h_tiles[no][:, at_h : at_h + PACK * CHUNK]),
+                out=side_by_side(h_tiles[no][:, at_h : at_h + PACK * CHUNK], PACK),
                 in0=row_by_row(bank[:]),
                 in1=row_by_row(pos_sb[np_][:, :, at_pos : at_pos + CHUNK]),
                 op=ADD,
@@ -185,7 +171,7 @@ def tile_picked_embpos_none_e_kernel(tc, xT, w1, w2, pos, offs, out):
         def second_layer(no):
             lo, hi = OUT_PIECES[no]
             codes, scales = quantize(h_tiles[no][:], "h%d" % lo)
-            bank = banks.tile([P, hi - lo], F32, name="bank")
+            bank = out_banks.tile([P, hi - lo], F32, name="out_bank")
             nc.tensor.matmul_mx(
                 out=bank[:],
                 lhsT=w2_codes[:].bitcast(FP8X4),
@@ -200,10 +186,21 @@ def tile_picked_embpos_none_e_kernel(tc, xT, w1, w2, pos, offs, out):
             queue = nc.scalar if hi == S else nc.sync
             queue.dma_start(out=out[:, lo:hi], in_=result[:])
 
-        h_sums = [first_layer(c) for c in range(S // CHUNK)]
+        chunks = S // CHUNK
+        h_sums = []
+
+        def open_chunk(c):
+            h_sums.append(banks.tile([P, PACK, CHUNK], F32, name="bank"))
+            first_layer_pass(c, 0, h_sums[c])
+
+        for c in range(LEAD):
+            open_chunk(c)
         done = 0
-        for c in range(S // CHUNK):
+        for c in range(chunks):
+            first_layer_pass(c, 1, h_sums[c])
             add_pos(c, h_sums[c])
+            if c + LEAD < chunks:
+                open_chunk(c + LEAD)
             if OUT_PIECES[done][1] <= c * CHUNK:
                 second_layer(done)
                 done = done + 1

@@ -27,8 +27,9 @@ X_LOADS = [
     [(0, 1024, 0), (1024, 2048, 672)],
     [(0, 1024, 0), (1024, 2048, 672)],
     [(0, 1024, 0), (1024, 2048, 288)],
-    [(0, 1024, 0), (1024, 1536, 512), (1536, 2048, 288)],
+    [(0, 512, 0), (512, 1536, 400), (1536, 2048, 336)],
 ]
+LIST_PIECES = [[(0, 256), (256, 512), (512, 1024)]] * 2
 POS_PIECES = [(0, 512), (512, 768), (768, 1024)]
 OUT_PIECES = [(0, 256), (256, 512), (512, 768), (768, 896), (896, 1024)]
 
@@ -92,26 +93,35 @@ def tile_picked_embpos_none_e_kernel(tc, xT, w1, w2, pos, offs, out):
                 if share < hi - lo:
                     scalar_copy(side_by_side(pairs[:, 2 * (lo + share) : 2 * hi], 2), row_by_row(raw[:, :, share:]))
                 if share > 0:
-                    nc.vector.tensor_copy(
-                        out=side_by_side(pairs[:, 2 * lo : 2 * (lo + share)], 2), in_=row_by_row(raw[:, :, :share])
-                    )
+                    into = pairs[:, 2 * lo : 2 * (lo + share)]
+                    if (n, lo) == (3, 512):
+                        nc.gpsimd.tensor_copy(
+                            out=into.rearrange("p (w e) -> p w e", e=2), in_=raw[:, :, :share].rearrange("p e w -> p w e")
+                        )
+                    else:
+                        nc.vector.tensor_copy(out=side_by_side(into, 2), in_=row_by_row(raw[:, :, :share]))
             return pairs
 
         halves = [(0, S // 2), (S // 2, S)]
 
         def weave_x(z):
-            picked = [tile([P, 2, hi - lo], U32, "picked%d_%d" % (z, lo)) for lo, hi in halves]
+            picked = [tile([P, 2, hi - lo], U32, "picked%d_%d" % (z, lo)) for lo, hi in LIST_PIECES[z]]
             for u in range(2):
                 pairs = round_pair(2 * z + u)
-                for (lo, hi), into in zip(halves, picked):
+                for (lo, hi), into in zip(LIST_PIECES[z], picked):
                     nc.vector.tensor_copy(
                         out=into[:, u, :], in_=pairs[:].bitcast(U32).indirect(offsets[:, lo // GROUP : hi // GROUP])
                     )
             woven = [tile([P, PACK * (hi - lo)], BF16, "woven%d_%d" % (z, lo)) for lo, hi in halves]
-            for into, words in zip(woven, picked):
-                nc.vector.tensor_copy(
-                    out=side_by_side(into[:].bitcast(I32), 2), in_=row_by_row(words[:].bitcast(I32))
-                )
+            for (lo, hi), words in zip(LIST_PIECES[z], picked):
+                half, at = divmod(lo, S // 2)
+                into = woven[half][:, PACK * at : PACK * (at + hi - lo)]
+                if half == 0:
+                    nc.gpsimd.tensor_copy(
+                        out=into.bitcast(U32).rearrange("p (s u) -> p s u", u=2), in_=words[:].rearrange("p u s -> p s u")
+                    )
+                else:
+                    nc.vector.tensor_copy(out=side_by_side(into.bitcast(I32), 2), in_=row_by_row(words[:].bitcast(I32)))
             return woven
 
         x_mx = [[quantize(values[:], "x0_%d" % n) for n, values in enumerate(weave_x(0))]]

@@ -24,10 +24,10 @@ RUN = 2
 LEAD = 3
 
 X_LOADS = [
-    [(0, 1024, 0), (1024, 2048, 672)],
-    [(0, 1024, 0), (1024, 2048, 672)],
-    [(0, 1024, 0), (1024, 2048, 288)],
-    [(0, 512, 0), (512, 1536, 400), (1536, 2048, 336)],
+    [(0, 1024, "vector", 0), (1024, 2048, "vector", 672)],
+    [(0, 1024, "gpsimd", 384), (1024, 2048, "vector", 688)],
+    [(0, 1024, "vector", 0), (1024, 2048, "vector", 144)],
+    [(0, 1024, "gpsimd", 416), (1024, 1536, "gpsimd", 224), (1536, 2048, "vector", 352)],
 ]
 LIST_PIECES = [[(0, 256), (256, 512), (512, 1024)]] * 2
 POS_PIECES = [(0, 512), (512, 768), (768, 1024)]
@@ -66,7 +66,7 @@ def tile_picked_embpos_none_e_kernel(tc, xT, w1, w2, pos, offs, out):
             z, u = divmod(n, 2)
             rows = xT[z * K_PASS : (z + 1) * K_PASS, :].rearrange("(p j) w -> p j w", j=PACK)[:, 2 * u : 2 * u + 2, :]
             raws = []
-            for lo, hi, share in pieces:
+            for lo, hi, helper, share in pieces:
                 raw = tile([P, 2, hi - lo], F32, "x_raw%d_%d" % (n, lo))
                 nc.sync.dma_start(out=raw[:], in_=rows[:, :, lo:hi])
                 raws.append(raw)
@@ -89,12 +89,12 @@ def tile_picked_embpos_none_e_kernel(tc, xT, w1, w2, pos, offs, out):
 
         def round_pair(n):
             pairs = tile([P, 2 * T], BF16, "pairs%d" % n)
-            for raw, (lo, hi, share) in zip(x_raw[n], X_LOADS[n]):
+            for raw, (lo, hi, helper, share) in zip(x_raw[n], X_LOADS[n]):
                 if share < hi - lo:
                     scalar_copy(side_by_side(pairs[:, 2 * (lo + share) : 2 * hi], 2), row_by_row(raw[:, :, share:]))
                 if share > 0:
                     into = pairs[:, 2 * lo : 2 * (lo + share)]
-                    if (n, lo) == (3, 512):
+                    if helper == "gpsimd":
                         nc.gpsimd.tensor_copy(
                             out=into.rearrange("p (w e) -> p w e", e=2), in_=raw[:, :, :share].rearrange("p e w -> p w e")
                         )
@@ -132,11 +132,14 @@ def tile_picked_embpos_none_e_kernel(tc, xT, w1, w2, pos, offs, out):
             for pair in range(2):
                 dealt = grouped[pair][:].rearrange("p (t m j) -> p m j t", t=2, j=PACK)
                 source = w1_raw[z][:].rearrange("p j (m t) -> p m j t", t=PACK)[:, :, :, 2 * pair : 2 * pair + 2]
-                scalar_copy(dealt, source)
+                if z == 1 and pair == 1:
+                    nc.vector.tensor_copy(out=dealt, in_=source)
+                else:
+                    scalar_copy(dealt, source)
             return [quantize(grouped[pair][:], "w1_%d%d" % (z, pair)) for pair in range(2)]
 
         w1_mx = [quantize_w1(0)]
-        x_mx.append([quantize(woven1[0][:], "x1_0", "w1_raw0")])
+        x_mx.append([quantize(woven1[0][:], "x1_0", "w1_grouped00")])
         w1_mx.append(quantize_w1(1))
         x_mx[1].append(quantize(woven1[1][:], "x1_1", "w1_grouped11"))
 

@@ -30,7 +30,7 @@ X_LOADS = [
     [(0, 1024, "gpsimd", 416), (1024, 1536, "gpsimd", 224), (1536, 2048, "vector", 352)],
 ]
 LIST_PIECES = [[(0, 256), (256, 512), (512, 1024)]] * 2
-POS_PIECES = [(0, 512), (512, 768), (768, 1024)]
+POS_PIECES = [(0, 512), (512, 768), (768, 896), (896, 1024)]
 OUT_PIECES = [(0, 256), (256, 512), (512, 768), (768, 896), (896, 1024)]
 
 

@@ -30,7 +30,7 @@ X_LOADS = [
     [(0, 1024, "gpsimd", 416), (1024, 1536, "gpsimd", 224), (1536, 2048, "vector", 352)],
 ]
 LIST_PIECES = [[(0, 256), (256, 512), (512, 1024)]] * 2
-POS_PIECES = [(0, 512), (512, 768), (768, 896), (896, 1024)]
+POS_PIECES = [(0, 256), (256, 512), (512, 768), (768, 896), (896, 1024)]
 OUT_PIECES = [(0, 256), (256, 512), (512, 768), (768, 896), (896, 1024)]
 
 
@@ -78,14 +78,15 @@ def tile_picked_embpos_none_e_kernel(tc, xT, w1, w2, pos, offs, out):
             raw = tile([P, PACK, H], F32, "w1_raw%d" % z)
             nc.sync.dma_start(out=raw[:], in_=w1[z * K_PASS : (z + 1) * K_PASS, :].rearrange("(p j) c -> p j c", j=PACK))
             w1_raw.append(raw)
-        w2_raw = tile([P, PACK, N], F32, "w2_raw")
-        nc.sync.dma_start(out=w2_raw[:], in_=w2.rearrange("(p j) c -> p j c", j=PACK))
         pos_rows = pos.rearrange("(p t) s -> p t s", t=PACK)
         pos_sb = []
         for n, (lo, hi) in enumerate(POS_PIECES):
             piece = tile([P, PACK, hi - lo], F32, "pos%d" % n)
             nc.sync.dma_start(out=piece[:], in_=pos_rows[:, :, lo:hi])
             pos_sb.append(piece)
+            if n == 0:
+                w2_raw = tile([P, PACK, N], F32, "w2_raw")
+                nc.sync.dma_start(out=w2_raw[:], in_=w2.rearrange("(p j) c -> p j c", j=PACK))
 
         def round_pair(n):
             pairs = tile([P, 2 * T], BF16, "pairs%d" % n)
@@ -145,7 +146,6 @@ def tile_picked_embpos_none_e_kernel(tc, xT, w1, w2, pos, offs, out):
 
         w2_grouped = tile([P, N * PACK], BF16, "w2_grouped")
         scalar_copy(side_by_side(w2_grouped[:], PACK), row_by_row(w2_raw[:]))
-        w2_codes, w2_scales = quantize(w2_grouped[:], "w2")
 
         def find(pieces, col):
             return [n for n, (lo, hi) in enumerate(pieces) if lo <= col < hi][0]
@@ -214,6 +214,8 @@ def tile_picked_embpos_none_e_kernel(tc, xT, w1, w2, pos, offs, out):
             add_pos(c, h_sums[c])
             if c + LEAD < chunks:
                 open_chunk(c + LEAD)
+            if c == 1:
+                w2_codes, w2_scales = quantize(w2_grouped[:], "w2")
             if OUT_PIECES[done][1] <= c * CHUNK:
                 second_layer(done)
                 done = done + 1

@@ -38,8 +38,8 @@ def tile_picked_embpos_none_e_kernel(tc, xT, w1, w2, pos, offs, out):
     nc = tc.nc
     with ExitStack() as ctx:
         keep = ctx.enter_context(tc.tile_pool(name="keep", bufs=1))
-        banks = ctx.enter_context(tc.psum_pool(name="banks", bufs=LEAD))
-        out_banks = ctx.enter_context(tc.psum_pool(name="out_banks", bufs=4))
+        banks = ctx.enter_context(tc.psum_pool(name="banks", bufs=6))
+        out_banks = ctx.enter_context(tc.psum_pool(name="out_banks", bufs=2))
 
         def tile(shape, dtype, name, tag=""):
             return keep.tile(shape, dtype, name=name, tag=tag or name, align_bytes=64)
@@ -103,8 +103,6 @@ def tile_picked_embpos_none_e_kernel(tc, xT, w1, w2, pos, offs, out):
                         nc.vector.tensor_copy(out=side_by_side(into, 2), in_=row_by_row(raw[:, :, :share]))
             return pairs
 
-        halves = [(0, S // 2), (S // 2, S)]
-
         def weave_x(z):
             picked = [tile([P, 2, hi - lo], U32, "picked%d_%d" % (z, lo)) for lo, hi in LIST_PIECES[z]]
             for u in range(2):
@@ -113,20 +111,24 @@ def tile_picked_embpos_none_e_kernel(tc, xT, w1, w2, pos, offs, out):
                     nc.vector.tensor_copy(
                         out=into[:, u, :], in_=pairs[:].bitcast(U32).indirect(offsets[:, lo // GROUP : hi // GROUP])
                     )
-            woven = [tile([P, PACK * (hi - lo)], BF16, "woven%d_%d" % (z, lo)) for lo, hi in halves]
-            for (lo, hi), words in zip(LIST_PIECES[z], picked):
-                half, at = divmod(lo, S // 2)
-                into = woven[half][:, PACK * at : PACK * (at + hi - lo)]
-                if half == 0:
-                    nc.gpsimd.tensor_copy(
-                        out=into.bitcast(U32).rearrange("p (s u) -> p s u", u=2), in_=words[:].rearrange("p u s -> p s u")
-                    )
-                else:
-                    nc.vector.tensor_copy(out=side_by_side(into.bitcast(I32), 2), in_=row_by_row(words[:].bitcast(I32)))
-            return woven
+            first = tile([P, PACK * S // 2], BF16, "woven%d_0" % z)
+            for (lo, hi), words in zip(LIST_PIECES[z][:2], picked):
+                nc.gpsimd.tensor_copy(
+                    out=first[:, PACK * lo : PACK * hi].bitcast(U32).rearrange("p (s u) -> p s u", u=2),
+                    in_=words[:].rearrange("p u s -> p s u"),
+                )
+            return first, picked[2]
 
-        x_mx = [[quantize(values[:], "x0_%d" % n) for n, values in enumerate(weave_x(0))]]
-        woven1 = weave_x(1)
+        def weave_second_half(words, name, tag=""):
+            second = tile([P, PACK * S // 2], BF16, name, tag)
+            nc.vector.tensor_copy(out=side_by_side(second[:].bitcast(I32), 2), in_=row_by_row(words[:].bitcast(I32)))
+            return second
+
+        first, words = weave_x(0)
+        second = weave_second_half(words, "woven0_1")
+        x_mx = [[quantize(first[:], "x0_0"), quantize(second[:], "x0_1")]]
+        first, words = weave_x(1)
+        x_mx.append([quantize(first[:], "x1_0")])
 
         def quantize_w1(z):
             grouped = [tile([P, 2 * P * PACK], BF16, "w1_grouped%d%d" % (z, pair)) for pair in range(2)]
@@ -140,9 +142,9 @@ def tile_picked_embpos_none_e_kernel(tc, xT, w1, w2, pos, offs, out):
             return [quantize(grouped[pair][:], "w1_%d%d" % (z, pair)) for pair in range(2)]
 
         w1_mx = [quantize_w1(0)]
-        x_mx.append([quantize(woven1[0][:], "x1_0", "w1_grouped00")])
+        second = weave_second_half(words, "woven1_1", "w1_grouped00")
         w1_mx.append(quantize_w1(1))
-        x_mx[1].append(quantize(woven1[1][:], "x1_1", "w1_grouped11"))
+        x_mx[1].append(quantize(second[:], "x1_1", "w1_grouped11"))
 
         w2_grouped = tile([P, N * PACK], BF16, "w2_grouped")
         scalar_copy(side_by_side(w2_grouped[:], PACK), row_by_row(w2_raw[:]))
@@ -152,7 +154,7 @@ def tile_picked_embpos_none_e_kernel(tc, xT, w1, w2, pos, offs, out):
 
         h_tiles = [tile([P, PACK * (hi - lo)], BF16, "h%d" % lo) for lo, hi in OUT_PIECES]
 
-        def first_layer_pass(c, z, bank):
+        def first_layer_pass(c, z, bank, opens):
             half, at = divmod(c * CHUNK, S // 2)
             x_codes, x_scales = x_mx[z][half]
             for t in range(PACK):
@@ -164,8 +166,8 @@ def tile_picked_embpos_none_e_kernel(tc, xT, w1, w2, pos, offs, out):
                     lhsT_scale=w_scales[:, m],
                     rhs=x_codes[:, at : at + CHUNK].bitcast(FP8X4),
                     rhs_scale=x_scales[:, at : at + CHUNK],
-                    start=(z == 0 and t == 0),
-                    stop=(z == 1 and t == PACK - 1),
+                    start=(opens and t == 0),
+                    stop=(not opens and t == PACK - 1),
                 )
 
         def add_pos(c, bank):
@@ -202,18 +204,20 @@ def tile_picked_embpos_none_e_kernel(tc, xT, w1, w2, pos, offs, out):
         chunks = S // CHUNK
         h_sums = []
 
-        def open_chunk(c):
+        def open_chunk(c, z):
             h_sums.append(banks.tile([P, PACK, CHUNK], F32, name="bank"))
-            first_layer_pass(c, 0, h_sums[c])
+            first_layer_pass(c, z, h_sums[c], True)
 
         for c in range(LEAD):
-            open_chunk(c)
+            open_chunk(c, 0)
         done = 0
         for c in range(chunks):
-            first_layer_pass(c, 1, h_sums[c])
+            if c < LEAD:
+                first_layer_pass(c, 1, h_sums[c], False)
+            else:
+                open_chunk(c, 1)
+                first_layer_pass(c, 0, h_sums[c], False)
             add_pos(c, h_sums[c])
-            if c + LEAD < chunks:
-                open_chunk(c + LEAD)
             if c == 1:
                 w2_codes, w2_scales = quantize(w2_grouped[:], "w2")
             if OUT_PIECES[done][1] <= c * CHUNK:

@@ -24,13 +24,13 @@ RUN = 2
 LEAD = 3
 
 X_LOADS = [
-    [(0, 1024, "vector", 0), (1024, 2048, "vector", 672)],
-    [(0, 1024, "gpsimd", 384), (1024, 2048, "vector", 688)],
-    [(0, 1024, "vector", 0), (1024, 2048, "vector", 144)],
-    [(0, 1024, "gpsimd", 416), (1024, 1536, "gpsimd", 224), (1536, 2048, "vector", 352)],
+    [(0, 2048, "vector", 1360)],
+    [(0, 2048, "vector", 1360)],
+    [(0, 1024, "vector", 0), (1024, 2048, "vector", 560)],
+    [(0, 1024, "gpsimd", 288), (1024, 1536, "vector", 256), (1536, 2048, "vector", 352)],
 ]
 LIST_PIECES = [[(0, 256), (256, 512), (512, 1024)]] * 2
-POS_PIECES = [(0, 256), (256, 512), (512, 768), (768, 896), (896, 1024)]
+POS_PIECES = [(0, 384), (384, 768), (768, 1024)]
 OUT_PIECES = [(0, 256), (256, 512), (512, 768), (768, 896), (896, 1024)]
 
 
@@ -84,7 +84,7 @@ def tile_picked_embpos_none_e_kernel(tc, xT, w1, w2, pos, offs, out):
             piece = tile([P, PACK, hi - lo], F32, "pos%d" % n)
             nc.sync.dma_start(out=piece[:], in_=pos_rows[:, :, lo:hi])
             pos_sb.append(piece)
-            if n == 0:
+            if n == 1:
                 w2_raw = tile([P, PACK, N], F32, "w2_raw")
                 nc.sync.dma_start(out=w2_raw[:], in_=w2.rearrange("(p j) c -> p j c", j=PACK))
 
@@ -103,31 +103,38 @@ def tile_picked_embpos_none_e_kernel(tc, xT, w1, w2, pos, offs, out):
                         nc.vector.tensor_copy(out=side_by_side(into, 2), in_=row_by_row(raw[:, :, :share]))
             return pairs
 
-        def weave_x(z):
-            picked = [tile([P, 2, hi - lo], U32, "picked%d_%d" % (z, lo)) for lo, hi in LIST_PIECES[z]]
-            for u in range(2):
-                pairs = round_pair(2 * z + u)
-                for (lo, hi), into in zip(LIST_PIECES[z], picked):
-                    nc.vector.tensor_copy(
-                        out=into[:, u, :], in_=pairs[:].bitcast(U32).indirect(offsets[:, lo // GROUP : hi // GROUP])
-                    )
+        def gather(pairs, lo, hi, into):
+            nc.vector.tensor_copy(out=into, in_=pairs[:].bitcast(U32).indirect(offsets[:, lo // GROUP : hi // GROUP]))
+
+        def weave_on_gpsimd(into, words):
+            nc.gpsimd.tensor_copy(out=into.rearrange("p (s u) -> p s u", u=2), in_=words.rearrange("p u s -> p s u"))
+
+        def gather_first_pair(z):
+            picked = tile([P, 2 * S], U32, "picked%d" % z)
+            gather(round_pair(2 * z), 0, S, picked[:, :S])
+            return picked
+
+        def gather_second_pair(z, picked):
+            pairs = round_pair(2 * z + 1)
+            for lo, hi in LIST_PIECES[z]:
+                gather(pairs, lo, hi, picked[:, S + lo : S + hi])
+            both = picked[:].rearrange("p (u s) -> p u s", u=2)
             first = tile([P, PACK * S // 2], BF16, "woven%d_0" % z)
-            for (lo, hi), words in zip(LIST_PIECES[z][:2], picked):
-                nc.gpsimd.tensor_copy(
-                    out=first[:, PACK * lo : PACK * hi].bitcast(U32).rearrange("p (s u) -> p s u", u=2),
-                    in_=words[:].rearrange("p u s -> p s u"),
-                )
-            return first, picked[2]
+            for lo, hi in LIST_PIECES[z][:2]:
+                into = first[:, PACK * lo : PACK * hi].bitcast(U32)
+                if lo == 0 and z == 1:
+                    nc.scalar.copy(out=side_by_side(into, 2), in_=row_by_row(both[:, :, lo:hi]))
+                else:
+                    weave_on_gpsimd(into, both[:, :, lo:hi])
+            return first, both[:, :, S // 2 :]
 
-        def weave_second_half(words, name, tag=""):
-            second = tile([P, PACK * S // 2], BF16, name, tag)
-            nc.vector.tensor_copy(out=side_by_side(second[:].bitcast(I32), 2), in_=row_by_row(words[:].bitcast(I32)))
-            return second
-
-        first, words = weave_x(0)
-        second = weave_second_half(words, "woven0_1")
-        x_mx = [[quantize(first[:], "x0_0"), quantize(second[:], "x0_1")]]
-        first, words = weave_x(1)
+        first, words = gather_second_pair(0, gather_first_pair(0))
+        x_mx = [[quantize(first[:], "x0_0")]]
+        picked = gather_first_pair(1)
+        second = tile([P, PACK * S // 2], BF16, "woven0_1", "x_raw2_1024")
+        weave_on_gpsimd(second[:].bitcast(U32), words)
+        x_mx[0].append(quantize(second[:], "x0_1"))
+        first, last_words = gather_second_pair(1, picked)
         x_mx.append([quantize(first[:], "x1_0")])
 
         def quantize_w1(z):
@@ -142,7 +149,8 @@ def tile_picked_embpos_none_e_kernel(tc, xT, w1, w2, pos, offs, out):
             return [quantize(grouped[pair][:], "w1_%d%d" % (z, pair)) for pair in range(2)]
 
         w1_mx = [quantize_w1(0)]
-        second = weave_second_half(words, "woven1_1", "w1_grouped00")
+        second = tile([P, PACK * S // 2], BF16, "woven1_1", "w1_grouped00")
+        nc.vector.tensor_copy(out=side_by_side(second[:].bitcast(I32), 2), in_=row_by_row(last_words.bitcast(I32)))
         w1_mx.append(quantize_w1(1))
         x_mx[1].append(quantize(second[:], "x1_1", "w1_grouped11"))
 
@@ -183,9 +191,14 @@ def tile_picked_embpos_none_e_kernel(tc, xT, w1, w2, pos, offs, out):
                 op=ADD,
             )
 
+        h_mx = []
+
+        def quantize_h(no):
+            h_mx.append(quantize(h_tiles[no][:], "h%d" % OUT_PIECES[no][0]))
+
         def second_layer(no):
             lo, hi = OUT_PIECES[no]
-            codes, scales = quantize(h_tiles[no][:], "h%d" % lo)
+            codes, scales = h_mx[no]
             bank = out_banks.tile([P, hi - lo], F32, name="out_bank")
             nc.tensor.matmul_mx(
                 out=bank[:],
@@ -211,6 +224,7 @@ def tile_picked_embpos_none_e_kernel(tc, xT, w1, w2, pos, offs, out):
         for c in range(LEAD):
             open_chunk(c, 0)
         done = 0
+        stored = 0
         for c in range(chunks):
             if c < LEAD:
                 first_layer_pass(c, 1, h_sums[c], False)
@@ -218,10 +232,15 @@ def tile_picked_embpos_none_e_kernel(tc, xT, w1, w2, pos, offs, out):
                 open_chunk(c, 1)
                 first_layer_pass(c, 0, h_sums[c], False)
             add_pos(c, h_sums[c])
-            if c == 1:
+            if c == 4:
                 w2_codes, w2_scales = quantize(w2_grouped[:], "w2")
             if OUT_PIECES[done][1] <= c * CHUNK:
-                second_layer(done)
+                quantize_h(done)
                 done = done + 1
+            if c >= 4:
+                for no in range(stored, done):
+                    second_layer(no)
+                stored = done
         for no in range(done, len(OUT_PIECES)):
+            quantize_h(no)
             second_layer(no)

@@ -21,7 +21,8 @@ K_PASS = P * PACK
 CHUNK = 128
 GROUP = 16
 RUN = 2
-LEAD = 3
+LEAD = 2
+BANKS = 6
 
 X_LOADS = [
     [(0, 2048, "vector", 1360)],
@@ -162,20 +163,23 @@ def tile_picked_embpos_none_e_kernel(tc, xT, w1, w2, pos, offs, out):
 
         h_tiles = [tile([P, PACK * (hi - lo)], BF16, "h%d" % lo) for lo, hi in OUT_PIECES]
 
-        def first_layer_pass(c, z, bank, opens):
+        h_sums = []
+
+        def first_layer(c, steps, opens, closes):
             half, at = divmod(c * CHUNK, S // 2)
-            x_codes, x_scales = x_mx[z][half]
-            for t in range(PACK):
+            passes = [(z, t) for z, pair in steps for t in (2 * pair, 2 * pair + 1)]
+            for z, t in passes:
+                x_codes, x_scales = x_mx[z][half]
                 w_codes, w_scales = w1_mx[z][t // 2]
                 m = slice((t % 2) * P, (t % 2 + 1) * P)
                 nc.tensor.matmul_mx(
-                    out=bank[:, t, :],
+                    out=h_sums[c][:, t, :],
                     lhsT=w_codes[:, m].bitcast(FP8X4),
                     lhsT_scale=w_scales[:, m],
                     rhs=x_codes[:, at : at + CHUNK].bitcast(FP8X4),
                     rhs_scale=x_scales[:, at : at + CHUNK],
-                    start=(opens and t == 0),
-                    stop=(not opens and t == PACK - 1),
+                    start=(opens and (z, t) == passes[0]),
+                    stop=(closes and (z, t) == passes[-1]),
                 )
 
         def add_pos(c, bank):
@@ -215,22 +219,27 @@ def tile_picked_embpos_none_e_kernel(tc, xT, w1, w2, pos, offs, out):
             queue.dma_start(out=out[:, lo:hi], in_=result[:])
 
         chunks = S // CHUNK
-        h_sums = []
 
-        def open_chunk(c, z):
+        def new_bank():
             h_sums.append(banks.tile([P, PACK, CHUNK], F32, name="bank"))
-            first_layer_pass(c, z, h_sums[c], True)
 
+        for c in range(BANKS):
+            new_bank()
+            first_layer(c, [(0, 0)], True, False)
         for c in range(LEAD):
-            open_chunk(c, 0)
+            first_layer(c, [(0, 1)], False, False)
         done = 0
         stored = 0
         for c in range(chunks):
-            if c < LEAD:
-                first_layer_pass(c, 1, h_sums[c], False)
+            if c == 0:
+                first_layer(c, [(1, 1), (1, 0)], False, True)
+            elif c < LEAD:
+                first_layer(c, [(1, 0), (1, 1)], False, True)
+            elif c < BANKS:
+                first_layer(c, [(1, 0), (1, 1), (0, 1)], False, True)
             else:
-                open_chunk(c, 1)
-                first_layer_pass(c, 0, h_sums[c], False)
+                new_bank()
+                first_layer(c, [(1, 0), (1, 1), (0, 1), (0, 0)], True, True)
             add_pos(c, h_sums[c])
             if c == 4:
                 w2_codes, w2_scales = quantize(w2_grouped[:], "w2")

@@ -22,13 +22,14 @@ CHUNK = 128
 GROUP = 16
 RUN = 2
 LEAD = 2
-BANKS = 6
+BANKS = 4
+W1_ON_VECTOR = 64
 
 X_LOADS = [
     [(0, 2048, "vector", 1360)],
     [(0, 2048, "vector", 1360)],
     [(0, 1024, "vector", 0), (1024, 2048, "vector", 560)],
-    [(0, 1024, "gpsimd", 288), (1024, 1536, "vector", 256), (1536, 2048, "vector", 352)],
+    [(0, 1024, "gpsimd", 432), (1024, 1536, "vector", 176), (1536, 2048, "vector", 352)],
 ]
 LIST_PIECES = [[(0, 256), (256, 512), (512, 1024)]] * 2
 POS_PIECES = [(0, 384), (384, 768), (768, 1024)]
@@ -133,7 +134,7 @@ def tile_picked_embpos_none_e_kernel(tc, xT, w1, w2, pos, offs, out):
         x_mx = [[quantize(first[:], "x0_0")]]
         picked = gather_first_pair(1)
         second = tile([P, PACK * S // 2], BF16, "woven0_1", "x_raw2_1024")
-        weave_on_gpsimd(second[:].bitcast(U32), words)
+        nc.scalar.copy(out=side_by_side(second[:].bitcast(U32), 2), in_=row_by_row(words))
         x_mx[0].append(quantize(second[:], "x0_1"))
         first, last_words = gather_second_pair(1, picked)
         x_mx.append([quantize(first[:], "x1_0")])
@@ -143,8 +144,9 @@ def tile_picked_embpos_none_e_kernel(tc, xT, w1, w2, pos, offs, out):
             for pair in range(2):
                 dealt = grouped[pair][:].rearrange("p (t m j) -> p m j t", t=2, j=PACK)
                 source = w1_raw[z][:].rearrange("p j (m t) -> p m j t", t=PACK)[:, :, :, 2 * pair : 2 * pair + 2]
-                if z == 1 and pair == 1:
-                    nc.vector.tensor_copy(out=dealt, in_=source)
+                if z == 1:
+                    nc.vector.tensor_copy(out=dealt[:, :W1_ON_VECTOR], in_=source[:, :W1_ON_VECTOR])
+                    scalar_copy(dealt[:, W1_ON_VECTOR:], source[:, W1_ON_VECTOR:])
                 else:
                     scalar_copy(dealt, source)
             return [quantize(grouped[pair][:], "w1_%d%d" % (z, pair)) for pair in range(2)]
@@ -203,7 +205,7 @@ def tile_picked_embpos_none_e_kernel(tc, xT, w1, w2, pos, offs, out):
         def second_layer(no):
             lo, hi = OUT_PIECES[no]
             codes, scales = h_mx[no]
-            bank = out_banks.tile([P, hi - lo], F32, name="out_bank")
+            bank = (out_banks if no < 3 else banks).tile([P, hi - lo], F32, name="bank")
             nc.tensor.matmul_mx(
                 out=bank[:],
                 lhsT=w2_codes[:].bitcast(FP8X4),
@@ -232,14 +234,14 @@ def tile_picked_embpos_none_e_kernel(tc, xT, w1, w2, pos, offs, out):
         stored = 0
         for c in range(chunks):
             if c == 0:
-                first_layer(c, [(1, 1), (1, 0)], False, True)
-            elif c < LEAD:
                 first_layer(c, [(1, 0), (1, 1)], False, True)
+            elif c < LEAD:
+                first_layer(c, [(1, 1), (1, 0)], False, True)
             elif c < BANKS:
-                first_layer(c, [(1, 0), (1, 1), (0, 1)], False, True)
+                first_layer(c, [(1, 1), (1, 0), (0, 1)], False, True)
             else:
                 new_bank()
-                first_layer(c, [(1, 0), (1, 1), (0, 1), (0, 0)], True, True)
+                first_layer(c, [(1, 1), (1, 0), (0, 1), (0, 0)], True, True)
             add_pos(c, h_sums[c])
             if c == 4:
                 w2_codes, w2_scales = quantize(w2_grouped[:], "w2")

@@ -8,7 +8,6 @@ FLOPS = 2 * K * H * S + 2 * H * N * S
 F32 = mybir.dt.float32
 BF16 = mybir.dt.bfloat16
 U32 = mybir.dt.uint32
-I32 = mybir.dt.int32
 U16 = mybir.dt.uint16
 U8 = mybir.dt.uint8
 FP8X4 = mybir.dt.float8_e4m3fn_x4
@@ -21,17 +20,12 @@ K_PASS = P * PACK
 CHUNK = 128
 GROUP = 16
 RUN = 2
+HALF = S // 2
+QUARTER = S // 4
 LEAD = 2
 BANKS = 4
-W1_ON_VECTOR = 64
+W1_ON_VECTOR = [[0, 48], [80, 80]]
 
-X_LOADS = [
-    [(0, 2048, "vector", 1360)],
-    [(0, 2048, "vector", 1360)],
-    [(0, 1024, "vector", 0), (1024, 2048, "vector", 560)],
-    [(0, 1024, "gpsimd", 432), (1024, 1536, "vector", 176), (1536, 2048, "vector", 352)],
-]
-LIST_PIECES = [[(0, 256), (256, 512), (512, 1024)]] * 2
 POS_PIECES = [(0, 384), (384, 768), (768, 1024)]
 OUT_PIECES = [(0, 256), (256, 512), (512, 768), (768, 896), (896, 1024)]
 
@@ -56,6 +50,9 @@ def tile_picked_embpos_none_e_kernel(tc, xT, w1, w2, pos, offs, out):
         def scalar_copy(out, in_):
             nc.scalar.activation(out=out, in_=in_, func=COPY)
 
+        def vector_copy(out, in_):
+            nc.vector.tensor_copy(out=out, in_=in_)
+
         def side_by_side(ap, rows):
             return ap.rearrange("p (c i j) -> p c j i", i=RUN, j=rows)
 
@@ -63,18 +60,19 @@ def tile_picked_embpos_none_e_kernel(tc, xT, w1, w2, pos, offs, out):
             return ap.rearrange("p j (c i) -> p c j i", i=RUN)
 
         offsets = tile([P, S // GROUP], U16, "offsets")
-        x_raw = []
-        for n, pieces in enumerate(X_LOADS):
-            z, u = divmod(n, 2)
-            rows = xT[z * K_PASS : (z + 1) * K_PASS, :].rearrange("(p j) w -> p j w", j=PACK)[:, 2 * u : 2 * u + 2, :]
-            raws = []
-            for lo, hi, helper, share in pieces:
-                raw = tile([P, 2, hi - lo], F32, "x_raw%d_%d" % (n, lo))
-                nc.sync.dma_start(out=raw[:], in_=rows[:, :, lo:hi])
-                raws.append(raw)
-            x_raw.append(raws)
-            if n == 0:
+        x_rows = [xT[z * K_PASS : (z + 1) * K_PASS, :].rearrange("(p j) w -> p j w", j=PACK) for z in range(2)]
+        x_pairs = []
+        for u in range(2):
+            raw = tile([P, 2 * T], F32, "x_pair%d" % u)
+            nc.sync.dma_start(out=raw[:].rearrange("p (j w) -> p j w", j=2), in_=x_rows[0][:, 2 * u : 2 * u + 2, :])
+            x_pairs.append(raw)
+            if u == 0:
                 nc.sync.dma_start(offsets[:], offs)
+        x_planes = []
+        for j in range(PACK):
+            raw = tile([P, T], F32, "x_plane%d" % j)
+            nc.sync.dma_start(out=raw[:], in_=x_rows[1][:, j, :])
+            x_planes.append(raw)
         w1_raw = []
         for z in range(2):
             raw = tile([P, PACK, H], F32, "w1_raw%d" % z)
@@ -90,72 +88,56 @@ def tile_picked_embpos_none_e_kernel(tc, xT, w1, w2, pos, offs, out):
                 w2_raw = tile([P, PACK, N], F32, "w2_raw")
                 nc.sync.dma_start(out=w2_raw[:], in_=w2.rearrange("(p j) c -> p j c", j=PACK))
 
-        def round_pair(n):
-            pairs = tile([P, 2 * T], BF16, "pairs%d" % n)
-            for raw, (lo, hi, helper, share) in zip(x_raw[n], X_LOADS[n]):
-                if share < hi - lo:
-                    scalar_copy(side_by_side(pairs[:, 2 * (lo + share) : 2 * hi], 2), row_by_row(raw[:, :, share:]))
-                if share > 0:
-                    into = pairs[:, 2 * lo : 2 * (lo + share)]
-                    if helper == "gpsimd":
-                        nc.gpsimd.tensor_copy(
-                            out=into.rearrange("p (w e) -> p w e", e=2), in_=raw[:, :, :share].rearrange("p e w -> p w e")
-                        )
-                    else:
-                        nc.vector.tensor_copy(out=side_by_side(into, 2), in_=row_by_row(raw[:, :, :share]))
-            return pairs
+        warm = tile([P, 2], F32, "warm")
+        nc.vector.memset(warm[:, 0:1], 0.0)
+        scalar_copy(warm[:, 1:2], warm[:, 0:1])
 
-        def gather(pairs, lo, hi, into):
-            nc.vector.tensor_copy(out=into, in_=pairs[:].bitcast(U32).indirect(offsets[:, lo // GROUP : hi // GROUP]))
+        def gather(copy, window, lo, hi, into):
+            copy(into, window.indirect(offsets[:, lo // GROUP : hi // GROUP]))
 
-        def weave_on_gpsimd(into, words):
-            nc.gpsimd.tensor_copy(out=into.rearrange("p (s u) -> p s u", u=2), in_=words.rearrange("p u s -> p s u"))
+        def lay_pair(woven, u, picked):
+            vector_copy(side_by_side(woven, PACK)[:, :, 2 * u : 2 * u + 2, :], row_by_row(picked))
 
-        def gather_first_pair(z):
-            picked = tile([P, 2 * S], U32, "picked%d" % z)
-            gather(round_pair(2 * z), 0, S, picked[:, :S])
-            return picked
+        woven = [[tile([P, PACK * HALF], BF16, "woven%d%d" % (z, half)) for half in range(2)] for z in range(2)]
+        for u in range(2):
+            picked = tile([P, 2, S], F32, "picked0%d" % u)
+            gather(scalar_copy, x_pairs[u][:], 0, S, picked[:, 0, :])
+            gather(vector_copy, x_pairs[u][:, T:], 0, S, picked[:, 1, :])
+            for half in range(2):
+                lay_pair(woven[0][half][:], u, picked[:, :, half * HALF : (half + 1) * HALF])
+        x_mx = [[quantize(woven[0][half][:], "x0%d" % half) for half in range(2)]]
 
-        def gather_second_pair(z, picked):
-            pairs = round_pair(2 * z + 1)
-            for lo, hi in LIST_PIECES[z]:
-                gather(pairs, lo, hi, picked[:, S + lo : S + hi])
-            both = picked[:].rearrange("p (u s) -> p u s", u=2)
-            first = tile([P, PACK * S // 2], BF16, "woven%d_0" % z)
-            for lo, hi in LIST_PIECES[z][:2]:
-                into = first[:, PACK * lo : PACK * hi].bitcast(U32)
-                if lo == 0 and z == 1:
-                    nc.scalar.copy(out=side_by_side(into, 2), in_=row_by_row(both[:, :, lo:hi]))
-                else:
-                    weave_on_gpsimd(into, both[:, :, lo:hi])
-            return first, both[:, :, S // 2 :]
+        halves = [tile([P, 2, HALF], F32, "picked10_%d" % half) for half in range(2)]
+        for half in range(2):
+            gather(scalar_copy, x_planes[0][:], half * HALF, (half + 1) * HALF, halves[half][:, 0, :])
+        gather(scalar_copy, x_planes[1][:], 0, HALF, halves[0][:, 1, :])
+        gather(scalar_copy, x_planes[1][:], HALF, HALF + QUARTER, halves[1][:, 1, :QUARTER])
+        gather(vector_copy, x_planes[1][:], HALF + QUARTER, S, halves[1][:, 1, QUARTER:])
+        for half in range(2):
+            lay_pair(woven[1][half][:], 0, halves[half][:])
 
-        first, words = gather_second_pair(0, gather_first_pair(0))
-        x_mx = [[quantize(first[:], "x0_0")]]
-        picked = gather_first_pair(1)
-        second = tile([P, PACK * S // 2], BF16, "woven0_1", "x_raw2_1024")
-        nc.scalar.copy(out=side_by_side(second[:].bitcast(U32), 2), in_=row_by_row(words))
-        x_mx[0].append(quantize(second[:], "x0_1"))
-        first, last_words = gather_second_pair(1, picked)
-        x_mx.append([quantize(first[:], "x1_0")])
+        quarters = [tile([P, 2, QUARTER], F32, "picked11_%d" % q) for q in range(4)]
+        for j in range(2):
+            for q in range(4):
+                copy = vector_copy if q == 3 else scalar_copy
+                gather(copy, x_planes[2 + j][:], q * QUARTER, (q + 1) * QUARTER, quarters[q][:, j, :])
+        for q in (0, 3, 1, 2):
+            half, at = divmod(q * QUARTER, HALF)
+            lay_pair(woven[1][half][:, PACK * at : PACK * (at + QUARTER)], 1, quarters[q][:])
+        x_mx.append([quantize(woven[1][half][:], "x1%d" % half) for half in range(2)])
 
         def quantize_w1(z):
             grouped = [tile([P, 2 * P * PACK], BF16, "w1_grouped%d%d" % (z, pair)) for pair in range(2)]
             for pair in range(2):
                 dealt = grouped[pair][:].rearrange("p (t m j) -> p m j t", t=2, j=PACK)
                 source = w1_raw[z][:].rearrange("p j (m t) -> p m j t", t=PACK)[:, :, :, 2 * pair : 2 * pair + 2]
-                if z == 1:
-                    nc.vector.tensor_copy(out=dealt[:, :W1_ON_VECTOR], in_=source[:, :W1_ON_VECTOR])
-                    scalar_copy(dealt[:, W1_ON_VECTOR:], source[:, W1_ON_VECTOR:])
-                else:
-                    scalar_copy(dealt, source)
+                share = W1_ON_VECTOR[z][pair]
+                if share > 0:
+                    vector_copy(dealt[:, :share], source[:, :share])
+                scalar_copy(dealt[:, share:], source[:, share:])
             return [quantize(grouped[pair][:], "w1_%d%d" % (z, pair)) for pair in range(2)]
 
-        w1_mx = [quantize_w1(0)]
-        second = tile([P, PACK * S // 2], BF16, "woven1_1", "w1_grouped00")
-        nc.vector.tensor_copy(out=side_by_side(second[:].bitcast(I32), 2), in_=row_by_row(last_words.bitcast(I32)))
-        w1_mx.append(quantize_w1(1))
-        x_mx[1].append(quantize(second[:], "x1_1", "w1_grouped11"))
+        w1_mx = [quantize_w1(0), quantize_w1(1)]
 
         w2_grouped = tile([P, N * PACK], BF16, "w2_grouped")
         scalar_copy(side_by_side(w2_grouped[:], PACK), row_by_row(w2_raw[:]))

@@ -61,18 +61,15 @@ def tile_picked_embpos_none_e_kernel(tc, xT, w1, w2, pos, offs, out):
 
         offsets = tile([P, S // GROUP], U16, "offsets")
         x_rows = [xT[z * K_PASS : (z + 1) * K_PASS, :].rearrange("(p j) w -> p j w", j=PACK) for z in range(2)]
-        x_pairs = []
-        for u in range(2):
-            raw = tile([P, 2 * T], F32, "x_pair%d" % u)
-            nc.sync.dma_start(out=raw[:].rearrange("p (j w) -> p j w", j=2), in_=x_rows[0][:, 2 * u : 2 * u + 2, :])
-            x_pairs.append(raw)
-            if u == 0:
-                nc.sync.dma_start(offsets[:], offs)
-        x_planes = []
-        for j in range(PACK):
-            raw = tile([P, T], F32, "x_plane%d" % j)
-            nc.sync.dma_start(out=raw[:], in_=x_rows[1][:, j, :])
-            x_planes.append(raw)
+        x_pair = tile([P, 2 * T], F32, "x_pair")
+        nc.sync.dma_start(out=x_pair[:].rearrange("p (j w) -> p j w", j=2), in_=x_rows[0][:, 0:2, :])
+        nc.sync.dma_start(offsets[:], offs)
+        x_planes = {}
+        for n in range(2, 2 * PACK):
+            z, j = divmod(n, PACK)
+            raw = tile([P, T], F32, "x_plane%d" % n)
+            nc.sync.dma_start(out=raw[:], in_=x_rows[z][:, j, :])
+            x_planes[n] = raw
         w1_raw = []
         for z in range(2):
             raw = tile([P, PACK, H], F32, "w1_raw%d" % z)
@@ -98,33 +95,26 @@ def tile_picked_embpos_none_e_kernel(tc, xT, w1, w2, pos, offs, out):
         def lay_pair(woven, u, picked):
             vector_copy(side_by_side(woven, PACK)[:, :, 2 * u : 2 * u + 2, :], row_by_row(picked))
 
-        woven = [[tile([P, PACK * HALF], BF16, "woven%d%d" % (z, half)) for half in range(2)] for z in range(2)]
-        for u in range(2):
-            picked = tile([P, 2, S], F32, "picked0%d" % u)
-            gather(scalar_copy, x_pairs[u][:], 0, S, picked[:, 0, :])
-            gather(vector_copy, x_pairs[u][:, T:], 0, S, picked[:, 1, :])
-            for half in range(2):
-                lay_pair(woven[0][half][:], u, picked[:, :, half * HALF : (half + 1) * HALF])
-        x_mx = [[quantize(woven[0][half][:], "x0%d" % half) for half in range(2)]]
+        def shared_pair(woven, n, pieces):
+            picked = [tile([P, 2, hi - lo], F32, "picked%d_%d" % (n, lo)) for lo, hi, copy in pieces]
+            for j in range(2):
+                for into, (lo, hi, copy) in zip(picked, pieces):
+                    gather(copy, x_planes[n + j][:], lo, hi, into[:, j, :])
+            for into, (lo, hi, copy) in zip(picked, pieces):
+                lay_pair(woven[:, PACK * lo : PACK * hi], n // 2 % 2, into[:])
 
-        halves = [tile([P, 2, HALF], F32, "picked10_%d" % half) for half in range(2)]
-        for half in range(2):
-            gather(scalar_copy, x_planes[0][:], half * HALF, (half + 1) * HALF, halves[half][:, 0, :])
-        gather(scalar_copy, x_planes[1][:], 0, HALF, halves[0][:, 1, :])
-        gather(scalar_copy, x_planes[1][:], HALF, HALF + QUARTER, halves[1][:, 1, :QUARTER])
-        gather(vector_copy, x_planes[1][:], HALF + QUARTER, S, halves[1][:, 1, QUARTER:])
-        for half in range(2):
-            lay_pair(woven[1][half][:], 0, halves[half][:])
-
-        quarters = [tile([P, 2, QUARTER], F32, "picked11_%d" % q) for q in range(4)]
-        for j in range(2):
-            for q in range(4):
-                copy = vector_copy if q == 3 else scalar_copy
-                gather(copy, x_planes[2 + j][:], q * QUARTER, (q + 1) * QUARTER, quarters[q][:, j, :])
-        for q in (0, 3, 1, 2):
-            half, at = divmod(q * QUARTER, HALF)
-            lay_pair(woven[1][half][:, PACK * at : PACK * (at + QUARTER)], 1, quarters[q][:])
-        x_mx.append([quantize(woven[1][half][:], "x1%d" % half) for half in range(2)])
+        woven = [tile([P, PACK * S], BF16, "woven%d" % z) for z in range(2)]
+        picked = tile([P, 2, S], F32, "picked0")
+        gather(scalar_copy, x_pair[:], 0, S, picked[:, 0, :])
+        gather(vector_copy, x_pair[:, T:], 0, S, picked[:, 1, :])
+        lay_pair(woven[0][:], 0, picked[:])
+        wide = [(3 * QUARTER, S, vector_copy), (0, 3 * QUARTER, scalar_copy)]
+        shared_pair(woven[0], 2, wide)
+        x_mx = [[quantize(woven[0][:, PACK * half * HALF : PACK * (half + 1) * HALF], "x0%d" % half) for half in range(2)]]
+        shared_pair(woven[1], 4, wide)
+        fine = [(q * QUARTER, (q + 1) * QUARTER, vector_copy if q == 3 else scalar_copy) for q in (0, 3, 1, 2)]
+        shared_pair(woven[1], 6, fine)
+        x_mx.append([quantize(woven[1][:, PACK * half * HALF : PACK * (half + 1) * HALF], "x1%d" % half) for half in range(2)])
 
         def quantize_w1(z):
             grouped = [tile([P, 2 * P * PACK], BF16, "w1_grouped%d%d" % (z, pair)) for pair in range(2)]

@@ -114,7 +114,7 @@ def tile_picked_embpos_none_e_kernel(tc, xT, w1, w2, pos, offs, out):
         shared_pair(woven[1], 4, wide)
         fine = [(q * QUARTER, (q + 1) * QUARTER, vector_copy if q == 3 else scalar_copy) for q in (0, 3, 1, 2)]
         shared_pair(woven[1], 6, fine)
-        x_mx.append([quantize(woven[1][:, PACK * half * HALF : PACK * (half + 1) * HALF], "x1%d" % half) for half in range(2)])
+        x_mx.append([quantize(woven[1][:, : PACK * HALF], "x10")])
 
         def quantize_w1(z):
             grouped = [tile([P, 2 * P * PACK], BF16, "w1_grouped%d%d" % (z, pair)) for pair in range(2)]
@@ -128,6 +128,7 @@ def tile_picked_embpos_none_e_kernel(tc, xT, w1, w2, pos, offs, out):
             return [quantize(grouped[pair][:], "w1_%d%d" % (z, pair)) for pair in range(2)]
 
         w1_mx = [quantize_w1(0), quantize_w1(1)]
+        x_mx[1].append(quantize(woven[1][:, PACK * HALF :], "x11", "w1_grouped11"))
 
         w2_grouped = tile([P, N * PACK], BF16, "w2_grouped")
         scalar_copy(side_by_side(w2_grouped[:], PACK), row_by_row(w2_raw[:]))

@@ -19,7 +19,7 @@ PACK = 4
 K_PASS = P * PACK
 CHUNK = 128
 GROUP = 16
-RUN = 2
+RUN = 4
 HALF = S // 2
 QUARTER = S // 4
 LEAD = 2

@@ -110,11 +110,11 @@ def tile_picked_embpos_none_e_kernel(tc, xT, w1, w2, pos, offs, out):
         lay_pair(woven[0][:], 0, picked[:])
         wide = [(3 * QUARTER, S, vector_copy), (0, 3 * QUARTER, scalar_copy)]
         shared_pair(woven[0], 2, wide)
-        x_mx = [[quantize(woven[0][:, PACK * half * HALF : PACK * (half + 1) * HALF], "x0%d" % half) for half in range(2)]]
+        x_mx = [{lo: quantize(woven[0][:, PACK * lo : PACK * (lo + HALF)], "x0_%d" % lo) for lo in (0, HALF)}]
         shared_pair(woven[1], 4, wide)
         fine = [(q * QUARTER, (q + 1) * QUARTER, vector_copy if q == 3 else scalar_copy) for q in (0, 3, 1, 2)]
         shared_pair(woven[1], 6, fine)
-        x_mx.append([quantize(woven[1][:, : PACK * HALF], "x10")])
+        x_mx.append({lo: quantize(woven[1][:, PACK * lo : PACK * hi], "x1_%d" % lo) for lo, hi in ((0, HALF), (3 * QUARTER, S))})
 
         def quantize_w1(z):
             grouped = [tile([P, 2 * P * PACK], BF16, "w1_grouped%d%d" % (z, pair)) for pair in range(2)]
@@ -125,10 +125,17 @@ def tile_picked_embpos_none_e_kernel(tc, xT, w1, w2, pos, offs, out):
                 if share > 0:
                     vector_copy(dealt[:, :share], source[:, :share])
                 scalar_copy(dealt[:, share:], source[:, share:])
-            return [quantize(grouped[pair][:], "w1_%d%d" % (z, pair)) for pair in range(2)]
+            widths = [2, 2] if z == 0 else [2, 1, 1]
+            made = []
+            for n, width in enumerate(widths):
+                first = sum(widths[:n])
+                values = grouped[first // 2][:, (first % 2) * P * PACK : (first % 2 + width) * P * PACK]
+                codes, scales = quantize(values, "w1_%d%d" % (z, first))
+                made.extend((codes[:, t * P : (t + 1) * P], scales[:, t * P : (t + 1) * P]) for t in range(width))
+            return made
 
         w1_mx = [quantize_w1(0), quantize_w1(1)]
-        x_mx[1].append(quantize(woven[1][:, PACK * HALF :], "x11", "w1_grouped11"))
+        x_mx[1].setdefault(HALF, quantize(woven[1][:, PACK * HALF : PACK * 3 * QUARTER], "x1_%d" % HALF, "w1_grouped11"))
 
         w2_grouped = tile([P, N * PACK], BF16, "w2_grouped")
         scalar_copy(side_by_side(w2_grouped[:], PACK), row_by_row(w2_raw[:]))
@@ -141,16 +148,16 @@ def tile_picked_embpos_none_e_kernel(tc, xT, w1, w2, pos, offs, out):
         h_sums = []
 
         def first_layer(c, steps, opens, closes):
-            half, at = divmod(c * CHUNK, S // 2)
             passes = [(z, t) for z, pair in steps for t in (2 * pair, 2 * pair + 1)]
             for z, t in passes:
-                x_codes, x_scales = x_mx[z][half]
-                w_codes, w_scales = w1_mx[z][t // 2]
-                m = slice((t % 2) * P, (t % 2 + 1) * P)
+                lo = max(first for first in x_mx[z] if first <= c * CHUNK)
+                at = c * CHUNK - lo
+                x_codes, x_scales = x_mx[z][lo]
+                w_codes, w_scales = w1_mx[z][t]
                 nc.tensor.matmul_mx(
                     out=h_sums[c][:, t, :],
-                    lhsT=w_codes[:, m].bitcast(FP8X4),
-                    lhsT_scale=w_scales[:, m],
+                    lhsT=w_codes.bitcast(FP8X4),
+                    lhsT_scale=w_scales,
                     rhs=x_codes[:, at : at + CHUNK].bitcast(FP8X4),
                     rhs_scale=x_scales[:, at : at + CHUNK],
                     start=(opens and (z, t) == passes[0]),

@@ -101,6 +101,8 @@ def tile_picked_embpos_none_e_kernel(tc, xT, w1, w2, pos, offs, out):
                 for into, (lo, hi, copy) in zip(picked, pieces):
                     gather(copy, x_planes[n + j][:], lo, hi, into[:, j, :])
             for into, (lo, hi, copy) in zip(picked, pieces):
+                if (n, lo) == (6, 3 * QUARTER):
+                    x_mx.append({0: quantize(woven[:, : PACK * HALF], "x1_0")})
                 lay_pair(woven[:, PACK * lo : PACK * hi], n // 2 % 2, into[:])
 
         woven = [tile([P, PACK * S], BF16, "woven%d" % z) for z in range(2)]
@@ -112,9 +114,22 @@ def tile_picked_embpos_none_e_kernel(tc, xT, w1, w2, pos, offs, out):
         shared_pair(woven[0], 2, wide)
         x_mx = [{lo: quantize(woven[0][:, PACK * lo : PACK * (lo + HALF)], "x0_%d" % lo) for lo in (0, HALF)}]
         shared_pair(woven[1], 4, wide)
-        fine = [(q * QUARTER, (q + 1) * QUARTER, vector_copy if q == 3 else scalar_copy) for q in (0, 3, 1, 2)]
+        fine = [(q * QUARTER, (q + 1) * QUARTER, vector_copy if q == 0 else scalar_copy) for q in range(4)]
         shared_pair(woven[1], 6, fine)
-        x_mx.append({lo: quantize(woven[1][:, PACK * lo : PACK * hi], "x1_%d" % lo) for lo, hi in ((0, HALF), (3 * QUARTER, S))})
+        x_mx[1].setdefault(HALF, quantize(woven[1][:, PACK * HALF : PACK * 3 * QUARTER], "x1_%d" % HALF))
+
+        codes, scales = x_mx[1][0]
+        for width in (512, 256, 128):
+            unread = out_banks.tile([P, width], F32, name="bank")
+            nc.tensor.matmul_mx(
+                out=unread[:],
+                lhsT=codes[:, :P].bitcast(FP8X4),
+                lhsT_scale=scales[:, :P],
+                rhs=codes[:, :width].bitcast(FP8X4),
+                rhs_scale=scales[:, :width],
+                start=True,
+                stop=True,
+            )
 
         def quantize_w1(z):
             grouped = [tile([P, 2 * P * PACK], BF16, "w1_grouped%d%d" % (z, pair)) for pair in range(2)]
@@ -135,7 +150,7 @@ def tile_picked_embpos_none_e_kernel(tc, xT, w1, w2, pos, offs, out):
             return made
 
         w1_mx = [quantize_w1(0), quantize_w1(1)]
-        x_mx[1].setdefault(HALF, quantize(woven[1][:, PACK * HALF : PACK * 3 * QUARTER], "x1_%d" % HALF, "w1_grouped11"))
+        x_mx[1].setdefault(3 * QUARTER, quantize(woven[1][:, PACK * 3 * QUARTER :], "x1_%d" % (3 * QUARTER), "w1_grouped11"))
 
         w2_grouped = tile([P, N * PACK], BF16, "w2_grouped")
         scalar_copy(side_by_side(w2_grouped[:], PACK), row_by_row(w2_raw[:]))

@@ -24,7 +24,7 @@ HALF = S // 2
 QUARTER = S // 4
 LEAD = 2
 BANKS = 4
-W1_ON_VECTOR = [[0, 48], [80, 80]]
+W1_ON_VECTOR = [[0, 88], [72, 72]]
 
 POS_PIECES = [(0, 384), (384, 768), (768, 1024)]
 OUT_PIECES = [(0, 256), (256, 512), (512, 768), (768, 896), (896, 1024)]

@@ -38,7 +38,7 @@ def tile_picked_embpos_none_e_kernel(tc, xT, w1, w2, pos, offs, out):
         out_banks = ctx.enter_context(tc.psum_pool(name="out_banks", bufs=2))
 
         def tile(shape, dtype, name, tag=""):
-            return keep.tile(shape, dtype, name=name, tag=tag or name, align_bytes=64)
+            return keep.tile(shape, dtype, name=name, tag=tag or name, align_bytes=512)
 
         def quantize(values, name, tag=""):
             width = values.shape[1] // PACK

@@ -152,13 +152,11 @@ def tile_picked_embpos_none_e_kernel(tc, xT, w1, w2, pos, offs, out):
         w1_mx = [quantize_w1(0), quantize_w1(1)]
         x_mx[1].setdefault(3 * QUARTER, quantize(woven[1][:, PACK * 3 * QUARTER :], "x1_%d" % (3 * QUARTER), "w1_grouped11"))
 
-        w2_grouped = tile([P, N * PACK], BF16, "w2_grouped")
-        scalar_copy(side_by_side(w2_grouped[:], PACK), row_by_row(w2_raw[:]))
+        h_tiles = [tile([P, PACK * (hi - lo + (N if lo == 256 else 0))], BF16, "h%d" % lo) for lo, hi in OUT_PIECES]
+        scalar_copy(side_by_side(h_tiles[1][:, PACK * 256 :], PACK), row_by_row(w2_raw[:]))
 
         def find(pieces, col):
             return [n for n, (lo, hi) in enumerate(pieces) if lo <= col < hi][0]
-
-        h_tiles = [tile([P, PACK * (hi - lo)], BF16, "h%d" % lo) for lo, hi in OUT_PIECES]
 
         h_sums = []
 
@@ -200,13 +198,14 @@ def tile_picked_embpos_none_e_kernel(tc, xT, w1, w2, pos, offs, out):
         def second_layer(no):
             lo, hi = OUT_PIECES[no]
             codes, scales = h_mx[no]
+            w2_codes, w2_scales = h_mx[1]
             bank = (out_banks if no < 3 else banks).tile([P, hi - lo], F32, name="bank")
             nc.tensor.matmul_mx(
                 out=bank[:],
-                lhsT=w2_codes[:].bitcast(FP8X4),
-                lhsT_scale=w2_scales[:],
-                rhs=codes[:].bitcast(FP8X4),
-                rhs_scale=scales[:],
+                lhsT=w2_codes[:, 256:].bitcast(FP8X4),
+                lhsT_scale=w2_scales[:, 256:],
+                rhs=codes[:, : hi - lo].bitcast(FP8X4),
+                rhs_scale=scales[:, : hi - lo],
                 start=True,
                 stop=True,
             )
@@ -226,7 +225,6 @@ def tile_picked_embpos_none_e_kernel(tc, xT, w1, w2, pos, offs, out):
         for c in range(LEAD):
             first_layer(c, [(0, 1)], False, False)
         done = 0
-        stored = 0
         for c in range(chunks):
             if c == 0:
                 first_layer(c, [(1, 0), (1, 1)], False, True)
@@ -238,15 +236,10 @@ def tile_picked_embpos_none_e_kernel(tc, xT, w1, w2, pos, offs, out):
                 new_bank()
                 first_layer(c, [(1, 1), (1, 0), (0, 1), (0, 0)], True, True)
             add_pos(c, h_sums[c])
-            if c == 4:
-                w2_codes, w2_scales = quantize(w2_grouped[:], "w2")
             if OUT_PIECES[done][1] <= c * CHUNK:
                 quantize_h(done)
                 done = done + 1
-            if c >= 4:
-                for no in range(stored, done):
-                    second_layer(no)
-                stored = done
         for no in range(done, len(OUT_PIECES)):
             quantize_h(no)
+        for no in range(len(OUT_PIECES)):
             second_layer(no)

@@ -27,13 +27,14 @@ BANKS = 4
 W1_ON_VECTOR = [[0, 88], [72, 72]]
 
 POS_PIECES = [(0, 384), (384, 768), (768, 1024)]
-OUT_PIECES = [(0, 256), (256, 512), (512, 768), (768, 896), (896, 1024)]
+ON_GPSIMD = (88, 48)
 
 
 def tile_picked_embpos_none_e_kernel(tc, xT, w1, w2, pos, offs, out):
     nc = tc.nc
     with ExitStack() as ctx:
         keep = ctx.enter_context(tc.tile_pool(name="keep", bufs=1))
+        staged = ctx.enter_context(tc.tile_pool(name="staged", bufs=1))
         banks = ctx.enter_context(tc.psum_pool(name="banks", bufs=6))
         out_banks = ctx.enter_context(tc.psum_pool(name="out_banks", bufs=2))
 
@@ -152,8 +153,18 @@ def tile_picked_embpos_none_e_kernel(tc, xT, w1, w2, pos, offs, out):
         w1_mx = [quantize_w1(0), quantize_w1(1)]
         x_mx[1].setdefault(3 * QUARTER, quantize(woven[1][:, PACK * 3 * QUARTER :], "x1_%d" % (3 * QUARTER), "w1_grouped11"))
 
-        h_tiles = [tile([P, PACK * (hi - lo + (N if lo == 256 else 0))], BF16, "h%d" % lo) for lo, hi in OUT_PIECES]
-        scalar_copy(side_by_side(h_tiles[1][:, PACK * 256 :], PACK), row_by_row(w2_raw[:]))
+        size = 2 * PACK * CHUNK
+
+        def h_tile(name, chunks_wide, offset):
+            return staged.tile([P, chunks_wide * PACK * CHUNK], BF16, name=name, align_bytes=512, offset=offset)
+
+        h_at = {}
+
+        def stage(name, parts, offset):
+            whole = h_tile(name, len(parts), offset)
+            for n, part in enumerate(parts):
+                h_at[part] = whole[:, n * K_PASS : (n + 1) * K_PASS]
+            return whole
 
         def find(pieces, col):
             return [n for n, (lo, hi) in enumerate(pieces) if lo <= col < hi][0]
@@ -177,44 +188,53 @@ def tile_picked_embpos_none_e_kernel(tc, xT, w1, w2, pos, offs, out):
                     stop=(closes and (z, t) == passes[-1]),
                 )
 
-        def add_pos(c, bank):
+        def pos_of(c, lo, hi):
             first = c * CHUNK
             np_ = find(POS_PIECES, first)
             at_pos = first - POS_PIECES[np_][0]
-            no = find(OUT_PIECES, first)
-            at_h = PACK * (first - OUT_PIECES[no][0])
+            return pos_sb[np_][:, :, at_pos + lo : at_pos + hi]
+
+        def add_pos(c, lo):
             nc.vector.tensor_tensor(
-                out=side_by_side(h_tiles[no][:, at_h : at_h + PACK * CHUNK], PACK),
-                in0=row_by_row(bank[:]),
-                in1=row_by_row(pos_sb[np_][:, :, at_pos : at_pos + CHUNK]),
+                out=side_by_side(h_at[c][:, PACK * lo :], PACK),
+                in0=row_by_row(h_sums[c][:, :, lo:]),
+                in1=row_by_row(pos_of(c, lo, CHUNK)),
                 op=ADD,
             )
 
-        h_mx = []
+        def add_pos_on_gpsimd(c, hi, tag=""):
+            sums = tile([P, hi, PACK], F32, "sums%d" % c, tag)
+            nc.scalar.copy(out=sums[:], in_=h_sums[c][:, :, :hi].rearrange("p t s -> p s t"))
+            nc.gpsimd.tensor_tensor(
+                out=h_at[c][:, : PACK * hi].rearrange("p (s t) -> p s t", t=PACK),
+                in0=sums[:],
+                in1=pos_of(c, 0, hi).rearrange("p t s -> p s t"),
+                op=ADD,
+            )
 
-        def quantize_h(no):
-            h_mx.append(quantize(h_tiles[no][:], "h%d" % OUT_PIECES[no][0]))
+        h_codes = tile([P, S + N], U32, "h_codes")
+        h_scales = tile([P, S + N], U8, "h_scales")
+        codes_at = {c: n * CHUNK for n, c in enumerate((0, 1, 2, 3, "w2", 4, 5, 6, 7))}
 
-        def second_layer(no):
-            lo, hi = OUT_PIECES[no]
-            codes, scales = h_mx[no]
-            w2_codes, w2_scales = h_mx[1]
-            bank = (out_banks if no < 3 else banks).tile([P, hi - lo], F32, name="bank")
+        def quantize_h(values, c):
+            at, width = codes_at[c], values.shape[1] // PACK
+            nc.vector.quantize_mx(out=h_codes[:, at : at + width].bitcast(FP8X4), scales=h_scales[:, at : at + width], in_=values)
+
+        def second_layer(c, width, pool, queue):
+            at, w2_at = codes_at[c], codes_at["w2"]
+            bank = pool.tile([P, width], F32, name="bank")
             nc.tensor.matmul_mx(
                 out=bank[:],
-                lhsT=w2_codes[:, 256:].bitcast(FP8X4),
-                lhsT_scale=w2_scales[:, 256:],
-                rhs=codes[:, : hi - lo].bitcast(FP8X4),
-                rhs_scale=scales[:, : hi - lo],
+                lhsT=h_codes[:, w2_at : w2_at + N].bitcast(FP8X4),
+                lhsT_scale=h_scales[:, w2_at : w2_at + N],
+                rhs=h_codes[:, at : at + width].bitcast(FP8X4),
+                rhs_scale=h_scales[:, at : at + width],
                 start=True,
                 stop=True,
             )
-            result = tile([P, hi - lo], F32, "result%d" % lo)
+            result = tile([P, width], F32, "result%d" % c)
             nc.scalar.copy(out=result[:], in_=bank[:])
-            queue = nc.scalar if hi == S else nc.sync
-            queue.dma_start(out=out[:, lo:hi], in_=result[:])
-
-        chunks = S // CHUNK
+            queue.dma_start(out=out[:, c * CHUNK : c * CHUNK + width], in_=result[:])
 
         def new_bank():
             h_sums.append(banks.tile([P, PACK, CHUNK], F32, name="bank"))
@@ -224,8 +244,8 @@ def tile_picked_embpos_none_e_kernel(tc, xT, w1, w2, pos, offs, out):
             first_layer(c, [(0, 0)], True, False)
         for c in range(LEAD):
             first_layer(c, [(0, 1)], False, False)
-        done = 0
-        for c in range(chunks):
+
+        def close_bank(c):
             if c == 0:
                 first_layer(c, [(1, 0), (1, 1)], False, True)
             elif c < LEAD:
@@ -235,11 +255,35 @@ def tile_picked_embpos_none_e_kernel(tc, xT, w1, w2, pos, offs, out):
             else:
                 new_bank()
                 first_layer(c, [(1, 1), (1, 0), (0, 1), (0, 0)], True, True)
-            add_pos(c, h_sums[c])
-            if OUT_PIECES[done][1] <= c * CHUNK:
-                quantize_h(done)
-                done = done + 1
-        for no in range(done, len(OUT_PIECES)):
-            quantize_h(no)
-        for no in range(len(OUT_PIECES)):
-            second_layer(no)
+
+        first_two = stage("h01", (0, 1), 0)
+        stage("h2", (2,), 2 * size)
+        for c in range(3):
+            close_bank(c)
+            add_pos(c, 0)
+        quantize_h(first_two[:], 0)
+        quantize_h(h_at[2], 2)
+        plain = stage("h45", (4, 5), 0)
+        shared = stage("h3", (3, "w2"), 2 * size)
+        close_bank(3)
+        add_pos_on_gpsimd(3, ON_GPSIMD[0])
+        scalar_copy(side_by_side(h_at["w2"], PACK), row_by_row(w2_raw[:]))
+        for c in (4, 5):
+            close_bank(c)
+            add_pos(c, 0)
+        add_pos(3, ON_GPSIMD[0])
+        quantize_h(plain[:], 4)
+        quantize_h(shared[:], 3)
+        stage("h7", (7,), 0)
+        stage("h6", (6,), 3 * size // 2)
+        close_bank(6)
+        close_bank(7)
+        add_pos_on_gpsimd(6, ON_GPSIMD[1], "w2_raw")
+        add_pos(7, 0)
+        add_pos(6, ON_GPSIMD[1])
+        quantize_h(h_at[7], 7)
+        quantize_h(h_at[6], 6)
+        for c in (0, 2, 4):
+            second_layer(c, 2 * CHUNK, out_banks, nc.sync)
+        second_layer(7, CHUNK, banks, nc.sync)
+        second_layer(6, CHUNK, banks, nc.scalar)

@@ -27,7 +27,7 @@ BANKS = 4
 W1_ON_VECTOR = [[0, 88], [72, 72]]
 
 POS_PIECES = [(0, 384), (384, 768), (768, 1024)]
-ON_GPSIMD = (88, 48)
+ON_GPSIMD = 80
 
 
 def tile_picked_embpos_none_e_kernel(tc, xT, w1, w2, pos, offs, out):
@@ -151,7 +151,7 @@ def tile_picked_embpos_none_e_kernel(tc, xT, w1, w2, pos, offs, out):
             return made
 
         w1_mx = [quantize_w1(0), quantize_w1(1)]
-        x_mx[1].setdefault(3 * QUARTER, quantize(woven[1][:, PACK * 3 * QUARTER :], "x1_%d" % (3 * QUARTER), "w1_grouped11"))
+        x_mx[1].setdefault(3 * QUARTER, quantize(woven[1][:, PACK * 3 * QUARTER :], "x1_%d" % (3 * QUARTER), "w1_raw1"))
 
         size = 2 * PACK * CHUNK
 
@@ -202,8 +202,8 @@ def tile_picked_embpos_none_e_kernel(tc, xT, w1, w2, pos, offs, out):
                 op=ADD,
             )
 
-        def add_pos_on_gpsimd(c, hi, tag=""):
-            sums = tile([P, hi, PACK], F32, "sums%d" % c, tag)
+        def add_pos_on_gpsimd(c, hi):
+            sums = tile([P, hi, PACK], F32, "sums%d" % c)
             nc.scalar.copy(out=sums[:], in_=h_sums[c][:, :, :hi].rearrange("p t s -> p s t"))
             nc.gpsimd.tensor_tensor(
                 out=h_at[c][:, : PACK * hi].rearrange("p (s t) -> p s t", t=PACK),
@@ -256,34 +256,32 @@ def tile_picked_embpos_none_e_kernel(tc, xT, w1, w2, pos, offs, out):
                 new_bank()
                 first_layer(c, [(1, 1), (1, 0), (0, 1), (0, 0)], True, True)
 
-        first_two = stage("h01", (0, 1), 0)
-        stage("h2", (2,), 2 * size)
+        stage("h0", (0,), 0)
+        before = stage("h12", (1, 2), 2 * size)
         for c in range(3):
             close_bank(c)
             add_pos(c, 0)
-        quantize_h(first_two[:], 0)
-        quantize_h(h_at[2], 2)
-        plain = stage("h45", (4, 5), 0)
-        shared = stage("h3", (3, "w2"), 2 * size)
+            if c == 1:
+                quantize_h(h_at[0], 0)
+        shared = stage("h3", (3, "w2"), 0)
+        plain = stage("h45", (4, 5), 4 * size)
         close_bank(3)
-        add_pos_on_gpsimd(3, ON_GPSIMD[0])
+        add_pos_on_gpsimd(3, ON_GPSIMD)
         scalar_copy(side_by_side(h_at["w2"], PACK), row_by_row(w2_raw[:]))
+        add_pos(3, ON_GPSIMD)
         for c in (4, 5):
             close_bank(c)
             add_pos(c, 0)
-        add_pos(3, ON_GPSIMD[0])
-        quantize_h(plain[:], 4)
+        quantize_h(before[:], 1)
         quantize_h(shared[:], 3)
-        stage("h7", (7,), 0)
-        stage("h6", (6,), 3 * size // 2)
-        close_bank(6)
-        close_bank(7)
-        add_pos_on_gpsimd(6, ON_GPSIMD[1], "w2_raw")
-        add_pos(7, 0)
-        add_pos(6, ON_GPSIMD[1])
-        quantize_h(h_at[7], 7)
-        quantize_h(h_at[6], 6)
+        quantize_h(plain[:], 4)
+        stage("h67", (6, 7), 2 * size)
+        for c in (6, 7):
+            close_bank(c)
+            add_pos(c, 0)
+        for c in (6, 7):
+            quantize_h(h_at[c], c)
         for c in (0, 2, 4):
             second_layer(c, 2 * CHUNK, out_banks, nc.sync)
-        second_layer(7, CHUNK, banks, nc.sync)
-        second_layer(6, CHUNK, banks, nc.scalar)
+        second_layer(6, CHUNK, banks, nc.sync)
+        second_layer(7, CHUNK, banks, nc.scalar)

@@ -27,7 +27,7 @@ BANKS = 4
 W1_ON_VECTOR = [[0, 88], [72, 72]]
 
 POS_PIECES = [(0, 384), (384, 768), (768, 1024)]
-ON_GPSIMD = 80
+ON_GPSIMD = (80, 48)
 
 
 def tile_picked_embpos_none_e_kernel(tc, xT, w1, w2, pos, offs, out):
@@ -202,8 +202,8 @@ def tile_picked_embpos_none_e_kernel(tc, xT, w1, w2, pos, offs, out):
                 op=ADD,
             )
 
-        def add_pos_on_gpsimd(c, hi):
-            sums = tile([P, hi, PACK], F32, "sums%d" % c)
+        def add_pos_on_gpsimd(c, hi, tag=""):
+            sums = tile([P, hi, PACK], F32, "sums%d" % c, tag)
             nc.scalar.copy(out=sums[:], in_=h_sums[c][:, :, :hi].rearrange("p t s -> p s t"))
             nc.gpsimd.tensor_tensor(
                 out=h_at[c][:, : PACK * hi].rearrange("p (s t) -> p s t", t=PACK),
@@ -266,22 +266,25 @@ def tile_picked_embpos_none_e_kernel(tc, xT, w1, w2, pos, offs, out):
         shared = stage("h3", (3, "w2"), 0)
         plain = stage("h45", (4, 5), 4 * size)
         close_bank(3)
-        add_pos_on_gpsimd(3, ON_GPSIMD)
+        add_pos_on_gpsimd(3, ON_GPSIMD[0])
         scalar_copy(side_by_side(h_at["w2"], PACK), row_by_row(w2_raw[:]))
-        add_pos(3, ON_GPSIMD)
+        add_pos(3, ON_GPSIMD[0])
         for c in (4, 5):
             close_bank(c)
             add_pos(c, 0)
         quantize_h(before[:], 1)
         quantize_h(shared[:], 3)
         quantize_h(plain[:], 4)
-        stage("h67", (6, 7), 2 * size)
-        for c in (6, 7):
-            close_bank(c)
-            add_pos(c, 0)
-        for c in (6, 7):
+        stage("h6", (6,), 0)
+        stage("h7", (7,), 2 * size)
+        close_bank(6)
+        close_bank(7)
+        add_pos_on_gpsimd(6, ON_GPSIMD[1], "w2_raw")
+        add_pos(7, 0)
+        add_pos(6, ON_GPSIMD[1])
+        for c in (7, 6):
             quantize_h(h_at[c], c)
         for c in (0, 2, 4):
             second_layer(c, 2 * CHUNK, out_banks, nc.sync)
-        second_layer(6, CHUNK, banks, nc.sync)
-        second_layer(7, CHUNK, banks, nc.scalar)
+        second_layer(7, CHUNK, banks, nc.sync)
+        second_layer(6, CHUNK, banks, nc.scalar)

@@ -24,7 +24,7 @@ HALF = S // 2
 QUARTER = S // 4
 LEAD = 2
 BANKS = 4
-W1_ON_VECTOR = [[0, 88], [72, 72]]
+W1_ON_VECTOR = [[0, 88], [72, 88]]
 
 POS_PIECES = [(0, 384), (384, 768), (768, 1024)]
 ON_GPSIMD = (80, 48)
@@ -258,14 +258,14 @@ def tile_picked_embpos_none_e_kernel(tc, xT, w1, w2, pos, offs, out):
 
         stage("h0", (0,), 0)
         before = stage("h12", (1, 2), 2 * size)
-        for c in range(3):
+        for c in (0, 1, 3, 2):
             close_bank(c)
+        for c in range(3):
             add_pos(c, 0)
             if c == 1:
                 quantize_h(h_at[0], 0)
         shared = stage("h3", (3, "w2"), 0)
         plain = stage("h45", (4, 5), 4 * size)
-        close_bank(3)
         add_pos_on_gpsimd(3, ON_GPSIMD[0])
         scalar_copy(side_by_side(h_at["w2"], PACK), row_by_row(w2_raw[:]))
         add_pos(3, ON_GPSIMD[0])
@@ -284,7 +284,8 @@ def tile_picked_embpos_none_e_kernel(tc, xT, w1, w2, pos, offs, out):
         add_pos(6, ON_GPSIMD[1])
         for c in (7, 6):
             quantize_h(h_at[c], c)
-        for c in (0, 2, 4):
+        for c in (0, 2):
             second_layer(c, 2 * CHUNK, out_banks, nc.sync)
+        second_layer(4, 2 * CHUNK, banks, nc.sync)
         second_layer(7, CHUNK, banks, nc.sync)
         second_layer(6, CHUNK, banks, nc.scalar)

@@ -24,7 +24,7 @@ HALF = S // 2
 QUARTER = S // 4
 LEAD = 2
 BANKS = 4
-W1_ON_VECTOR = [[0, 88], [72, 88]]
+W1_ON_VECTOR = [[64, 72], [72, 88]]
 
 POS_PIECES = [(0, 384), (384, 768), (768, 1024)]
 ON_GPSIMD = (80, 48)
@@ -102,8 +102,6 @@ def tile_picked_embpos_none_e_kernel(tc, xT, w1, w2, pos, offs, out):
                 for into, (lo, hi, copy) in zip(picked, pieces):
                     gather(copy, x_planes[n + j][:], lo, hi, into[:, j, :])
             for into, (lo, hi, copy) in zip(picked, pieces):
-                if (n, lo) == (6, 3 * QUARTER):
-                    x_mx.append({0: quantize(woven[:, : PACK * HALF], "x1_0")})
                 lay_pair(woven[:, PACK * lo : PACK * hi], n // 2 % 2, into[:])
 
         woven = [tile([P, PACK * S], BF16, "woven%d" % z) for z in range(2)]
@@ -115,9 +113,16 @@ def tile_picked_embpos_none_e_kernel(tc, xT, w1, w2, pos, offs, out):
         shared_pair(woven[0], 2, wide)
         x_mx = [{lo: quantize(woven[0][:, PACK * lo : PACK * (lo + HALF)], "x0_%d" % lo) for lo in (0, HALF)}]
         shared_pair(woven[1], 4, wide)
-        fine = [(q * QUARTER, (q + 1) * QUARTER, vector_copy if q == 0 else scalar_copy) for q in range(4)]
-        shared_pair(woven[1], 6, fine)
-        x_mx[1].setdefault(HALF, quantize(woven[1][:, PACK * HALF : PACK * 3 * QUARTER], "x1_%d" % HALF))
+        fine = [(q * QUARTER, (q + 1) * QUARTER, vector_copy if q == 0 else scalar_copy) for q in range(2)]
+        picked = [tile([P, 2, QUARTER], F32, "picked6_%d" % lo) for lo, hi, copy in fine]
+        for j in range(2):
+            for into, (lo, hi, copy) in zip(picked, fine):
+                gather(copy, x_planes[6 + j][:], lo, hi, into[:, j, :])
+            for lo in (HALF, 3 * QUARTER):
+                gather(scalar_copy, x_planes[6 + j][:], lo, lo + QUARTER, woven[1][:, PACK * lo + 2 + j : PACK * (lo + QUARTER) : PACK])
+        for into, (lo, hi, copy) in zip(picked, fine):
+            lay_pair(woven[1][:, PACK * lo : PACK * hi], 1, into[:])
+        x_mx.append({0: quantize(woven[1][:, : PACK * HALF], "x1_0")})
 
         codes, scales = x_mx[1][0]
         for width in (512, 256, 128):
@@ -150,7 +155,9 @@ def tile_picked_embpos_none_e_kernel(tc, xT, w1, w2, pos, offs, out):
                 made.extend((codes[:, t * P : (t + 1) * P], scales[:, t * P : (t + 1) * P]) for t in range(width))
             return made
 
-        w1_mx = [quantize_w1(0), quantize_w1(1)]
+        w1_mx = [quantize_w1(0)]
+        x_mx[1].setdefault(HALF, quantize(woven[1][:, PACK * HALF : PACK * 3 * QUARTER], "x1_%d" % HALF, "w1_raw0"))
+        w1_mx.append(quantize_w1(1))
         x_mx[1].setdefault(3 * QUARTER, quantize(woven[1][:, PACK * 3 * QUARTER :], "x1_%d" % (3 * QUARTER), "w1_raw1"))
 
         size = 2 * PACK * CHUNK

@@ -113,8 +113,8 @@ def tile_picked_embpos_none_e_kernel(tc, xT, w1, w2, pos, offs, out):
         shared_pair(woven[0], 2, wide)
         x_mx = [{lo: quantize(woven[0][:, PACK * lo : PACK * (lo + HALF)], "x0_%d" % lo) for lo in (0, HALF)}]
         shared_pair(woven[1], 4, wide)
-        fine = [(q * QUARTER, (q + 1) * QUARTER, vector_copy if q == 0 else scalar_copy) for q in range(2)]
-        picked = [tile([P, 2, QUARTER], F32, "picked6_%d" % lo) for lo, hi, copy in fine]
+        fine = [(0, CHUNK, vector_copy), (CHUNK, QUARTER, vector_copy), (QUARTER, HALF, scalar_copy)]
+        picked = [tile([P, 2, hi - lo], F32, "picked6_%d" % lo) for lo, hi, copy in fine]
         for j in range(2):
             for into, (lo, hi, copy) in zip(picked, fine):
                 gather(copy, x_planes[6 + j][:], lo, hi, into[:, j, :])

from contextlib import ExitStack

import concourse.mybir as mybir

K, T, S, H, N = 1024, 2048, 1024, 512, 128
FLOPS = 2 * K * H * S + 2 * H * N * S

F32 = mybir.dt.float32
BF16 = mybir.dt.bfloat16
U32 = mybir.dt.uint32
U16 = mybir.dt.uint16
U8 = mybir.dt.uint8
FP8X4 = mybir.dt.float8_e4m3fn_x4
ADD = mybir.AluOpType.add
COPY = mybir.ActivationFunctionType.Copy

P = 128
PACK = 4
K_PASS = P * PACK
CHUNK = 128
GROUP = 16
RUN = 4
HALF = S // 2
QUARTER = S // 4
LEAD = 2
BANKS = 4
W1_ON_VECTOR = [[64, 72], [72, 88]]

POS_PIECES = [(0, 384), (384, 768), (768, 1024)]
ON_GPSIMD = (80, 48)


def tile_picked_embpos_none_e_kernel(tc, xT, w1, w2, pos, offs, out):
    nc = tc.nc
    with ExitStack() as ctx:
        keep = ctx.enter_context(tc.tile_pool(name="keep", bufs=1))
        staged = ctx.enter_context(tc.tile_pool(name="staged", bufs=1))
        banks = ctx.enter_context(tc.psum_pool(name="banks", bufs=6))
        out_banks = ctx.enter_context(tc.psum_pool(name="out_banks", bufs=2))

        def tile(shape, dtype, name, tag=""):
            return keep.tile(shape, dtype, name=name, tag=tag or name, align_bytes=512)

        def quantize(values, name, tag=""):
            width = values.shape[1] // PACK
            codes = tile([P, width], U32, name + "_codes", tag)
            scales = tile([P, width], U8, name + "_scales")
            nc.vector.quantize_mx(out=codes[:].bitcast(FP8X4), scales=scales[:], in_=values)
            return codes, scales

        def scalar_copy(out, in_):
            nc.scalar.activation(out=out, in_=in_, func=COPY)

        def vector_copy(out, in_):
            nc.vector.tensor_copy(out=out, in_=in_)

        def side_by_side(ap, rows):
            return ap.rearrange("p (c i j) -> p c j i", i=RUN, j=rows)

        def row_by_row(ap):
            return ap.rearrange("p j (c i) -> p c j i", i=RUN)

        offsets = tile([P, S // GROUP], U16, "offsets")
        x_rows = [xT[z * K_PASS : (z + 1) * K_PASS, :].rearrange("(p j) w -> p j w", j=PACK) for z in range(2)]
        x_pair = tile([P, 2 * T], F32, "x_pair")
        nc.sync.dma_start(out=x_pair[:].rearrange("p (j w) -> p j w", j=2), in_=x_rows[0][:, 0:2, :])
        nc.sync.dma_start(offsets[:], offs)
        x_planes = {}
        for n in range(2, 2 * PACK):
            z, j = divmod(n, PACK)
            raw = tile([P, T], F32, "x_plane%d" % n)
            nc.sync.dma_start(out=raw[:], in_=x_rows[z][:, j, :])
            x_planes[n] = raw
        w1_raw = []
        for z in range(2):
            raw = tile([P, PACK, H], F32, "w1_raw%d" % z)
            nc.sync.dma_start(out=raw[:], in_=w1[z * K_PASS : (z + 1) * K_PASS, :].rearrange("(p j) c -> p j c", j=PACK))
            w1_raw.append(raw)
        pos_rows = pos.rearrange("(p t) s -> p t s", t=PACK)
        pos_sb = []
        for n, (lo, hi) in enumerate(POS_PIECES):
            piece = tile([P, PACK, hi - lo], F32, "pos%d" % n)
            nc.sync.dma_start(out=piece[:], in_=pos_rows[:, :, lo:hi])
            pos_sb.append(piece)
            if n == 1:
                w2_raw = tile([P, PACK, N], F32, "w2_raw")
                nc.sync.dma_start(out=w2_raw[:], in_=w2.rearrange("(p j) c -> p j c", j=PACK))

        warm = tile([P, 2], F32, "warm")
        nc.vector.memset(warm[:, 0:1], 0.0)
        scalar_copy(warm[:, 1:2], warm[:, 0:1])

        def gather(copy, window, lo, hi, into):
            copy(into, window.indirect(offsets[:, lo // GROUP : hi // GROUP]))

        def lay_pair(woven, u, picked):
            vector_copy(side_by_side(woven, PACK)[:, :, 2 * u : 2 * u + 2, :], row_by_row(picked))

        def shared_pair(woven, n, pieces):
            picked = [tile([P, 2, hi - lo], F32, "picked%d_%d" % (n, lo)) for lo, hi, copy in pieces]
            for j in range(2):
                for into, (lo, hi, copy) in zip(picked, pieces):
                    gather(copy, x_planes[n + j][:], lo, hi, into[:, j, :])
            for into, (lo, hi, copy) in zip(picked, pieces):
                lay_pair(woven[:, PACK * lo : PACK * hi], n // 2 % 2, into[:])

        woven = [tile([P, PACK * S], BF16, "woven%d" % z) for z in range(2)]
        picked = tile([P, 2, S], F32, "picked0")
        gather(scalar_copy, x_pair[:], 0, S, picked[:, 0, :])
        gather(vector_copy, x_pair[:, T:], 0, S, picked[:, 1, :])
        lay_pair(woven[0][:], 0, picked[:])
        wide = [(3 * QUARTER, S, vector_copy), (0, 3 * QUARTER, scalar_copy)]
        shared_pair(woven[0], 2, wide)
        x_mx = [{lo: quantize(woven[0][:, PACK * lo : PACK * (lo + HALF)], "x0_%d" % lo) for lo in (0, HALF)}]
        shared_pair(woven[1], 4, wide)
        fine = [(0, CHUNK, vector_copy), (CHUNK, QUARTER, vector_copy), (QUARTER, HALF, scalar_copy)]
        picked = [tile([P, 2, hi - lo], F32, "picked6_%d" % lo) for lo, hi, copy in fine]
        for j in range(2):
            for into, (lo, hi, copy) in zip(picked, fine):
                gather(copy, x_planes[6 + j][:], lo, hi, into[:, j, :])
            for lo in (HALF, 3 * QUARTER):
                gather(scalar_copy, x_planes[6 + j][:], lo, lo + QUARTER, woven[1][:, PACK * lo + 2 + j : PACK * (lo + QUARTER) : PACK])
        for into, (lo, hi, copy) in zip(picked, fine):
            lay_pair(woven[1][:, PACK * lo : PACK * hi], 1, into[:])
        x_mx.append({0: quantize(woven[1][:, : PACK * HALF], "x1_0")})

        codes, scales = x_mx[1][0]
        for width in (512, 256, 128):
            unread = out_banks.tile([P, width], F32, name="bank")
            nc.tensor.matmul_mx(
                out=unread[:],
                lhsT=codes[:, :P].bitcast(FP8X4),
                lhsT_scale=scales[:, :P],
                rhs=codes[:, :width].bitcast(FP8X4),
                rhs_scale=scales[:, :width],
                start=True,
                stop=True,
            )

        def quantize_w1(z):
            grouped = [tile([P, 2 * P * PACK], BF16, "w1_grouped%d%d" % (z, pair)) for pair in range(2)]
            for pair in range(2):
                dealt = grouped[pair][:].rearrange("p (t m j) -> p m j t", t=2, j=PACK)
                source = w1_raw[z][:].rearrange("p j (m t) -> p m j t", t=PACK)[:, :, :, 2 * pair : 2 * pair + 2]
                share = W1_ON_VECTOR[z][pair]
                if share > 0:
                    vector_copy(dealt[:, :share], source[:, :share])
                scalar_copy(dealt[:, share:], source[:, share:])
            widths = [2, 2] if z == 0 else [2, 1, 1]
            made = []
            for n, width in enumerate(widths):
                first = sum(widths[:n])
                values = grouped[first // 2][:, (first % 2) * P * PACK : (first % 2 + width) * P * PACK]
                codes, scales = quantize(values, "w1_%d%d" % (z, first))
                made.extend((codes[:, t * P : (t + 1) * P], scales[:, t * P : (t + 1) * P]) for t in range(width))
            return made

        w1_mx = [quantize_w1(0)]
        x_mx[1].setdefault(HALF, quantize(woven[1][:, PACK * HALF : PACK * 3 * QUARTER], "x1_%d" % HALF, "w1_raw0"))
        w1_mx.append(quantize_w1(1))
        x_mx[1].setdefault(3 * QUARTER, quantize(woven[1][:, PACK * 3 * QUARTER :], "x1_%d" % (3 * QUARTER), "w1_raw1"))

        size = 2 * PACK * CHUNK

        def h_tile(name, chunks_wide, offset):
            return staged.tile([P, chunks_wide * PACK * CHUNK], BF16, name=name, align_bytes=512, offset=offset)

        h_at = {}

        def stage(name, parts, offset):
            whole = h_tile(name, len(parts), offset)
            for n, part in enumerate(parts):
                h_at[part] = whole[:, n * K_PASS : (n + 1) * K_PASS]
            return whole

        def find(pieces, col):
            return [n for n, (lo, hi) in enumerate(pieces) if lo <= col < hi][0]

        h_sums = []

        def first_layer(c, steps, opens, closes):
            passes = [(z, t) for z, pair in steps for t in (2 * pair, 2 * pair + 1)]
            for z, t in passes:
                lo = max(first for first in x_mx[z] if first <= c * CHUNK)
                at = c * CHUNK - lo
                x_codes, x_scales = x_mx[z][lo]
                w_codes, w_scales = w1_mx[z][t]
                nc.tensor.matmul_mx(
                    out=h_sums[c][:, t, :],
                    lhsT=w_codes.bitcast(FP8X4),
                    lhsT_scale=w_scales,
                    rhs=x_codes[:, at : at + CHUNK].bitcast(FP8X4),
                    rhs_scale=x_scales[:, at : at + CHUNK],
                    start=(opens and (z, t) == passes[0]),
                    stop=(closes and (z, t) == passes[-1]),
                )

        def pos_of(c, lo, hi):
            first = c * CHUNK
            np_ = find(POS_PIECES, first)
            at_pos = first - POS_PIECES[np_][0]
            return pos_sb[np_][:, :, at_pos + lo : at_pos + hi]

        def add_pos(c, lo):
            nc.vector.tensor_tensor(
                out=side_by_side(h_at[c][:, PACK * lo :], PACK),
                in0=row_by_row(h_sums[c][:, :, lo:]),
                in1=row_by_row(pos_of(c, lo, CHUNK)),
                op=ADD,
            )

        def add_pos_on_gpsimd(c, hi, tag=""):
            sums = tile([P, hi, PACK], F32, "sums%d" % c, tag)
            nc.scalar.copy(out=sums[:], in_=h_sums[c][:, :, :hi].rearrange("p t s -> p s t"))
            nc.gpsimd.tensor_tensor(
                out=h_at[c][:, : PACK * hi].rearrange("p (s t) -> p s t", t=PACK),
                in0=sums[:],
                in1=pos_of(c, 0, hi).rearrange("p t s -> p s t"),
                op=ADD,
            )

        h_codes = tile([P, S + N], U32, "h_codes")
        h_scales = tile([P, S + N], U8, "h_scales")
        codes_at = {c: n * CHUNK for n, c in enumerate((0, 1, 2, 3, "w2", 4, 5, 6, 7))}

        def quantize_h(values, c):
            at, width = codes_at[c], values.shape[1] // PACK
            nc.vector.quantize_mx(out=h_codes[:, at : at + width].bitcast(FP8X4), scales=h_scales[:, at : at + width], in_=values)

        def second_layer(c, width, pool, queue):
            at, w2_at = codes_at[c], codes_at["w2"]
            bank = pool.tile([P, width], F32, name="bank")
            nc.tensor.matmul_mx(
                out=bank[:],
                lhsT=h_codes[:, w2_at : w2_at + N].bitcast(FP8X4),
                lhsT_scale=h_scales[:, w2_at : w2_at + N],
                rhs=h_codes[:, at : at + width].bitcast(FP8X4),
                rhs_scale=h_scales[:, at : at + width],
                start=True,
                stop=True,
            )
            result = tile([P, width], F32, "result%d" % c)
            nc.scalar.copy(out=result[:], in_=bank[:])
            queue.dma_start(out=out[:, c * CHUNK : c * CHUNK + width], in_=result[:])

        def new_bank():
            h_sums.append(banks.tile([P, PACK, CHUNK], F32, name="bank"))

        for c in range(BANKS):
            new_bank()
            first_layer(c, [(0, 0)], True, False)
        for c in range(LEAD):
            first_layer(c, [(0, 1)], False, False)

        def close_bank(c):
            if c == 0:
                first_layer(c, [(1, 0), (1, 1)], False, True)
            elif c < LEAD:
                first_layer(c, [(1, 1), (1, 0)], False, True)
            elif c < BANKS:
                first_layer(c, [(1, 1), (1, 0), (0, 1)], False, True)
            else:
                new_bank()
                first_layer(c, [(1, 1), (1, 0), (0, 1), (0, 0)], True, True)

        stage("h0", (0,), 0)
        before = stage("h12", (1, 2), 2 * size)
        for c in (0, 1, 3, 2):
            close_bank(c)
        for c in range(3):
            add_pos(c, 0)
            if c == 1:
                quantize_h(h_at[0], 0)
        shared = stage("h3", (3, "w2"), 0)
        plain = stage("h45", (4, 5), 4 * size)
        add_pos_on_gpsimd(3, ON_GPSIMD[0])
        scalar_copy(side_by_side(h_at["w2"], PACK), row_by_row(w2_raw[:]))
        add_pos(3, ON_GPSIMD[0])
        for c in (4, 5):
            close_bank(c)
            add_pos(c, 0)
        quantize_h(before[:], 1)
        quantize_h(shared[:], 3)
        quantize_h(plain[:], 4)
        stage("h6", (6,), 0)
        stage("h7", (7,), 2 * size)
        close_bank(6)
        close_bank(7)
        add_pos_on_gpsimd(6, ON_GPSIMD[1], "w2_raw")
        add_pos(7, 0)
        add_pos(6, ON_GPSIMD[1])
        for c in (7, 6):
            quantize_h(h_at[c], c)
        for c in (0, 2):
            second_layer(c, 2 * CHUNK, out_banks, nc.sync)
        second_layer(4, 2 * CHUNK, banks, nc.sync)
        second_layer(7, CHUNK, banks, nc.sync)
        second_layer(6, CHUNK, banks, nc.scalar)
